import numpy as np
import ml_dtypes


def mxq(x, axis, fmt="e4m3"):
    dtype, down = {"e4m3": (ml_dtypes.float8_e4m3fn, 7), "e5m2": (ml_dtypes.float8_e5m2, 14)}[fmt]
    v = np.moveaxis(np.asarray(x, np.float32).astype(ml_dtypes.bfloat16).astype(np.float64), axis, -1)
    blocks = v.reshape(v.shape[:-1] + (-1, 32))
    amax = np.abs(blocks).max(-1, keepdims=True)
    byte = np.maximum(np.where(amax > 0, np.frexp(amax)[1] - 1 + 127, 0) - down, 1)
    scale = np.exp2(byte - 127.0)
    codes = (blocks / scale).astype(np.float32).astype(dtype).astype(np.float64)
    return np.moveaxis((codes * scale).reshape(v.shape), -1, axis)


WIDE = False


def mx_kscale(k):
    if not WIDE:
        return np.ones(k)
    levels = np.array([10, -10, 5, -5, 0])
    if k % 512:
        return np.exp2(np.random.permutation(np.resize(levels, k // 32))).repeat(32)
    a = np.empty((k // 512, 16))
    for p in range(k // 512):
        a[p, :8] = np.random.permutation(np.resize(levels, 8))
        for g in range(8):
            far = levels[np.abs(levels - a[p, g]) >= 10]
            a[p, g + 8] = far[np.random.randint(len(far))]
    return np.exp2(a.ravel()).repeat(32)


def f64(x):
    return np.asarray(x).astype(np.float64)


def striped(idx):
    return np.tile(idx.reshape(-1, 16).T, (8, 1)).astype(np.uint16)


def unstriped(offs):
    return offs[:16].T.reshape(-1).astype(np.int64)


E2M1 = np.array([0.0, 0.5, 1.0, 1.5, 2.0, 3.0, 4.0, 6.0, -0.0, -0.5, -1.0, -1.5, -2.0, -3.0, -4.0, -6.0])


def pack_weight(w, fmt):
    k, n = w.shape
    w = f64(np.asarray(w, np.float32).astype(ml_dtypes.bfloat16)).reshape(k // 32, 32, n)
    amax = np.abs(w).max(1)
    if fmt == "e4m3":
        byte = np.frexp(amax)[1] - 1 + 127 - 7
    else:
        mant, ex = np.frexp(amax / 6.0)
        byte = np.where(mant > 0.5, ex, ex - 1) + 127
    byte = np.clip(np.where(amax > 0, byte, 1), 1, 254)
    scaled = (w * np.exp2(127.0 - byte)[:, None, :]).reshape(k, n).astype(np.float32)
    by_word = np.ascontiguousarray(scaled.reshape(k // 512, 128, 4, n).transpose(0, 1, 3, 2))
    if fmt == "e4m3":
        words = by_word.astype(ml_dtypes.float8_e4m3fn).view(np.uint8)
    else:
        c = by_word.astype(ml_dtypes.float4_e2m1fn).view(np.uint8) & 0xF
        words = (c[..., 0::2] | (c[..., 1::2] << 4)).reshape(k // 512, 128, 2 * n)
    return np.ascontiguousarray(words), np.ascontiguousarray(byte.astype(np.uint8).reshape(k // 512, 16, n))


def unpack_weight(words, scales, fmt):
    g, _, n = scales.shape
    words = np.ascontiguousarray(words).reshape(g, 128, n, -1)
    if fmt == "e4m3":
        vals = words.view(ml_dtypes.float8_e4m3fn).astype(np.float64)
    else:
        nib = np.empty((g, 128, n, 4), np.uint8)
        nib[..., 0::2] = words & 0xF
        nib[..., 1::2] = words >> 4
        vals = E2M1[nib]
    vals = vals * np.repeat(np.exp2(scales.astype(np.float64) - 127.0), 8, axis=1)[..., None]
    return vals.transpose(0, 1, 3, 2).reshape(g * 512, n)


def gelu(v):
    return 0.5 * v * (1.0 + np.tanh(np.sqrt(2.0 / np.pi) * (v + 0.044715 * v**3)))


K, K1, K2, T, S, H, T2, S2, T3, P = 1536, 1024, 512, 2048, 1024, 1024, 2048, 512, 2048, 1024

def setup_inputs():
    n = np.random.standard_normal
    s = mx_kscale(K)[:, None]
    u = mx_kscale(H)[:, None]
    tab_words, tab_scales = pack_weight(n((K, T)) * s, "e4m3")
    w4_words, w4_scales = pack_weight(n((K2, H)) / np.sqrt(K) / s[K1:], "e2m1")
    tab2_words, tab2_scales = pack_weight(1.5 * n((H, T3)) / np.sqrt(H) / u, "e4m3")
    return {
        "tab_words": tab_words, "tab_scales": tab_scales,
        "w1": (n((K1, H)) / np.sqrt(K) / s[:K1]).astype(np.float32),
        "w4_words": w4_words, "w4_scales": w4_scales,
        "gain": (np.exp(0.3 * n(H)) * u[:, 0]).astype(np.float32),
        "page0": (n((H, T2)) * u).astype(np.float32),
        "wgs": np.exp(0.3 * n((128, S))).astype(np.float32),
        "tab2_words": tab2_words, "tab2_scales": tab2_scales,
        "prior": n(S2).astype(np.float32),
        "offs": striped(np.random.permutation(T)[:S]),
        "offs2": striped(np.random.permutation(T3)[:S2]),
        "offs3": striped(np.random.permutation(T2)[:S]),
        "offs4": striped(np.random.permutation(T2)[:P]),
    }

def reference(tab_words, tab_scales, w1, w4_words, w4_scales, gain, page0, wgs,
              tab2_words, tab2_scales, prior, offs, offs2, offs3, offs4):
    v = unpack_weight(tab_words, tab_scales, "e4m3")[:, unstriped(offs)]
    w4 = unpack_weight(w4_words, w4_scales, "e2m1")
    pre = mxq(f64(w1), 0, "e4m3").T @ v[:K1] + w4.T @ v[K1:]
    h = f64(gain)[:, None] * np.tanh(pre)
    page = f64(page0).copy()
    page[:, unstriped(offs3)] = np.tile(f64(wgs), (H // 128, 1)) * h
    v2 = unpack_weight(tab2_words, tab2_scales, "e4m3")[:, unstriped(offs2)]
    e = v2.T @ mxq(page, 0, "e4m3")
    x = e[:, unstriped(offs4)] + f64(prior)[:, None]
    return 1.0 / (1.0 + np.exp(-x))

@@ -1,0 +1,307 @@
+from contextlib import ExitStack
+
+import concourse.mybir as mybir
+
+K1, K2, T, S, H, T2, S2, P_OUT = 1024, 512, 2048, 1024, 1024, 2048, 512, 1024
+FLOPS = 2 * (K1 + K2) * H * S + 2 * H * S2 * T2
+
+F32 = mybir.dt.float32
+BF16 = mybir.dt.bfloat16
+I32 = mybir.dt.int32
+U32 = mybir.dt.uint32
+U16 = mybir.dt.uint16
+U8 = mybir.dt.uint8
+FP8X4 = mybir.dt.float8_e4m3fn_x4
+FP4X4 = mybir.dt.float4_e2m1fn_x4
+ACT = mybir.ActivationFunctionType
+MULT = mybir.AluOpType.mult
+
+P = 128
+PACK = 4
+K_PASS = P * PACK
+BANK = 512
+GROUP = 16
+CHUNKS = T2 // BANK
+PLANES = H // P
+SCALAR_CHUNKS = 2
+VCOPY = ()
+TANH_TAG = ["tanh_a", "tanh_b", "tanh_c", "tanh_a", "tanh_b", "tanh_a", "tanh_b", "tanh_a"]
+
+
+def tile_list_opening_explorer_scores_kernel(
+    tc, tab_words, tab_scales, w1, w4_words, w4_scales, gain, page0, wgs,
+    tab2_words, tab2_scales, prior, offs, offs2, offs3, offs4, out,
+):
+    nc = tc.nc
+    with ExitStack() as ctx:
+        keep = ctx.enter_context(tc.tile_pool(name="keep", bufs=1))
+        psum = ctx.enter_context(tc.psum_pool(name="psum", bufs=1))
+
+        def sbuf(shape, dtype, name, tag=None, bufs=1):
+            return keep.tile(shape, dtype, name=name, tag=tag or name, bufs=bufs, align_bytes=64)
+
+        def load_list(src, name):
+            t = keep.tile(list(src.shape), U16, name=name, tag=name)
+            nc.sync.dma_start(t[:], src)
+            return t
+
+        def load_words(words, a, name):
+            t = sbuf([P, T], I32, name, "slab", 6)
+            nc.sync.dma_start(t[:], words[a].rearrange("p t i -> p (t i)").bitcast(I32))
+            return t
+
+        def load_w1(a, g):
+            t = sbuf([P, PACK, K_PASS], F32, "w1_raw_%d_%d" % (a, g), "slab", 6)
+            rows = w1[g * K_PASS:(g + 1) * K_PASS, a * K_PASS:(a + 1) * K_PASS]
+            nc.sync.dma_start(t[:], rows.rearrange("(p j) c -> p j c", j=PACK))
+            return t
+
+        def load_page(k):
+            a, i = divmod(k, PACK)
+            t = sbuf([P, T2], F32, "page_%d" % k, "page", 5)
+            rows = page0[a * K_PASS:(a + 1) * K_PASS, :].rearrange("(p i) t -> p i t", i=PACK)
+            nc.sync.dma_start(t[:], rows[:, i, :])
+            return t
+
+        def load_wgs(i):
+            t = sbuf([P, S], F32, "wgs_%d" % i)
+            rows = wgs.rearrange("(q i) j -> q i j", i=PACK)[:, i, :]
+            for quad in (0, 2, 1, 3):
+                nc.sync.dma_start(t[32 * quad:32 * quad + 32, :], rows)
+            return t
+
+        def scale_tile(width, name):
+            t = sbuf([P, width], U8, name)
+            nc.vector.memset(t[:].bitcast(I32), 0)
+            return t
+
+        def load_scales(t, scales, first, count, row, quad):
+            nc.sync.dma_start(
+                t[32 * quad + row:32 * quad + row + 4 * count, :].bitcast(I32),
+                scales[first:first + count, 4 * quad:4 * quad + 4, :].bitcast(I32),
+            )
+
+        def gather(dst, window, offsets, lo, hi):
+            nc.vector.tensor_copy(dst, window.indirect(offsets[:, lo // GROUP:hi // GROUP]))
+
+        tab_sc = scale_tile(T, "tab_sc")
+        w4_sc_raw = scale_tile(H, "w4_sc_raw")
+        tab2_sc = scale_tile(T, "tab2_sc")
+
+        idx = load_list(offs, "idx")
+        tab = {2: load_words(tab_words, 2, "tab_2")}
+        for quad in range(4):
+            load_scales(tab_sc, tab_scales, 0, 2, 4, quad)
+        w4_raw = sbuf([P, 2 * H], U8, "w4_raw")
+        nc.sync.dma_start(w4_raw[:].bitcast(I32), w4_words[0].bitcast(I32))
+        load_scales(tab_sc, tab_scales, 2, 1, 0, 0)
+        tab[0] = load_words(tab_words, 0, "tab_0")
+        for quad in range(1, 4):
+            load_scales(tab_sc, tab_scales, 2, 1, 0, quad)
+        w1_raw = {(0, 0): load_w1(0, 0)}
+        for quad in range(4):
+            load_scales(w4_sc_raw, w4_scales, 0, 1, 0, quad)
+        w1_raw[(0, 1)] = load_w1(0, 1)
+        tab[1] = load_words(tab_words, 1, "tab_1")
+        gain_sb = sbuf([P, 2, PACK], F32, "gain_sb")
+        nc.sync.dma_start(gain_sb[:], gain.rearrange("(a p i) -> p a i", p=P, i=PACK))
+        idx3 = load_list(offs3, "idx3")
+        wgs_sb = [load_wgs(0)]
+        page = [load_page(0)]
+        wgs_sb.append(load_wgs(1))
+        w1_raw[(1, 0)] = load_w1(1, 0)
+        page.append(load_page(1))
+        w1_raw[(1, 1)] = load_w1(1, 1)
+        for i in (2, 3):
+            wgs_sb.append(load_wgs(i))
+            page.append(load_page(i))
+        idx2 = load_list(offs2, "idx2")
+        for quad in range(4):
+            load_scales(tab2_sc, tab2_scales, 0, 2, 0, quad)
+        page.append(load_page(4))
+        idx4 = load_list(offs4, "idx4")
+        prior_sb = sbuf([P, S2 // P], F32, "prior_sb")
+        with nc.allow_non_contiguous_dma(reason="one prior value for each partition"):
+            nc.sync.dma_start(prior_sb[:], prior.rearrange("(n p) -> p n", p=P))
+        tab2 = [load_words(tab2_words, a, "tab2_%d" % a) for a in range(2)]
+        for k in range(5, PLANES):
+            page.append(load_page(k))
+
+        w4 = sbuf([P, 2 * H], U8, "w4")
+        nc.vector.tensor_copy(
+            w4[:].bitcast(U16).rearrange("p (a i m) -> p a m i", a=2, i=PACK),
+            w4_raw[:].bitcast(U16).rearrange("p (a m i) -> p a m i", a=2, i=PACK),
+        )
+        v = {a: sbuf([P, S], U32, "v_%d" % a) for a in range(3)}
+        v_sc = sbuf([P, S], U8, "v_sc")
+        w1_codes, w1_sc = {}, {}
+
+        def weave_w1(a, g):
+            t = sbuf([P, PACK * K_PASS], BF16, "w1_b_%d_%d" % (a, g), "woven_%d" % (2 * a + g))
+            nc.scalar.copy(
+                t[:].rearrange("p (i m j) -> p m j i", i=PACK, j=PACK),
+                w1_raw[(a, g)][:].rearrange("p j (m i) -> p m j i", i=PACK),
+            )
+            return t
+
+        def quantize_w1(a, g, woven):
+            if g == 0:
+                w1_codes[a] = sbuf([P, 2, K_PASS], U32, "w1_codes_%d" % a, "tanh_c" if a else None)
+            w1_codes[(a, g)] = w1_codes[a][:, g, :]
+            w1_sc[(a, g)] = sbuf([P, K_PASS], U8, "w1_sc_%d_%d" % (a, g))
+            nc.vector.quantize_mx(out=w1_codes[(a, g)].bitcast(FP8X4), scales=w1_sc[(a, g)][:], in_=woven[:])
+
+        gather(v[2][:], tab[2][:].bitcast(U32), idx, 0, S)
+        gather(v[0][:], tab[0][:].bitcast(U32), idx, 0, S)
+        gather(v_sc[:], tab_sc[:], idx, 0, S)
+        quantize_w1(0, 0, weave_w1(0, 0))
+        w4_sc = sbuf([P, H], U8, "w4_sc")
+        nc.vector.tensor_copy(
+            w4_sc[:].rearrange("p (a i m) -> p a m i", a=2, i=PACK),
+            w4_sc_raw[:].rearrange("p (a m i) -> p a m i", a=2, i=PACK),
+        )
+        quantize_w1(0, 1, weave_w1(0, 1))
+        for lo in range(0, S, BANK):
+            gather(v[1][:, lo:lo + BANK], tab[1][:].bitcast(U32), idx, lo, lo + BANK)
+
+        tanh_sb = {}
+
+        def encode(k, step=S):
+            a, i = divmod(k, PACK)
+            tanh_sb[k] = sbuf([P, S], F32, "tanh_%d" % k, TANH_TAG[k])
+            col = a * K_PASS + i * P
+            for lo in range(0, S, BANK):
+                js = slice(lo, lo + BANK)
+                bank = psum.tile([P, BANK], F32, name="bank", tag="bank_%d" % (2 * (k % 2) + (lo // BANK if k else 0)))
+                nc.tensor.matmul_mx(
+                    out=bank[:], lhsT=w4[:, 2 * col:2 * (col + P)].bitcast(FP4X4), lhsT_scale=w4_sc[:, col:col + P],
+                    rhs=v[2][:, js].bitcast(FP8X4), rhs_scale=v_sc[:, js], start=True, stop=False,
+                )
+                for g in range(2):
+                    nc.tensor.matmul_mx(
+                        out=bank[:], lhsT=w1_codes[(a, g)][:, i * P:(i + 1) * P].bitcast(FP8X4),
+                        lhsT_scale=w1_sc[(a, g)][:, i * P:(i + 1) * P],
+                        rhs=v[g][:, js].bitcast(FP8X4), rhs_scale=v_sc[4 * (g + 1):P, js],
+                        start=False, stop=(g == 1),
+                    )
+                if k == 0:
+                    raw = sbuf([P, BANK], F32, "tanh_raw", TANH_TAG[1 + lo // BANK])
+                    nc.scalar.activation(raw[:], bank[:], ACT.Tanh)
+                    nc.scalar.activation(tanh_sb[k][:, js], raw[:], ACT.Copy, scale=gain_sb[:, a, i:i + 1])
+                    continue
+                nc.scalar.activation(tanh_sb[k][:, js], bank[:], ACT.Tanh)
+                if (lo + BANK) % step == 0:
+                    part = tanh_sb[k][:, lo + BANK - step:lo + BANK]
+                    nc.scalar.activation(part, part, ACT.Copy, scale=gain_sb[:, a, i:i + 1])
+
+        def scatter(k, step):
+            for lo in range(0, S, step):
+                nc.vector.tensor_tensor(
+                    page[k][:].indirect(idx3[:, lo // GROUP:(lo + step) // GROUP]),
+                    tanh_sb[k][:, lo:lo + step], wgs_sb[k % PACK][:, lo:lo + step], MULT,
+                )
+
+        rounded, woven, codes, scales = {}, {}, {}, {}
+
+        def copy_on(engine, dst, src):
+            if engine == "scalar":
+                nc.scalar.copy(dst, src)
+            else:
+                nc.vector.tensor_copy(dst, src)
+
+        def round_plane(k, engine):
+            a, i = divmod(k, PACK)
+            for c in range(CHUNKS):
+                if i == 0:
+                    rounded[(a, c)] = sbuf([P, PACK, BANK], BF16, "rounded_%d_%d" % (a, c), "rounded_%d" % c)
+                copy_on(engine, rounded[(a, c)][:, i, :], page[k][:, c * BANK:(c + 1) * BANK])
+
+        def weave(a, c, engine):
+            woven[(a, c)] = sbuf([P, PACK * BANK], BF16, "woven_%d_%d" % (a, c), "woven_%d" % (c if a == 0 else 4 + c % SCALAR_CHUNKS))
+            copy_on(
+                engine,
+                woven[(a, c)][:].rearrange("p (t u i) -> p t i u", u=4, i=PACK),
+                rounded[(a, c)][:].rearrange("p i (t u) -> p t i u", u=4),
+            )
+
+        def quantize_page(a, c, dst):
+            codes[(a, c)] = dst
+            scales[(a, c)] = sbuf([P, BANK], U8, "page_sc_%d_%d" % (a, c))
+            nc.vector.quantize_mx(out=dst.bitcast(FP8X4), scales=scales[(a, c)][:], in_=woven[(a, c)][:])
+
+        encode(0, BANK)
+        encode(1)
+        encode(2)
+        scatter(0, BANK)
+        encode(3)
+        late_w1 = [weave_w1(1, 0)]
+        scatter(1, S)
+        round_plane(0, "scalar")
+        late_w1.append(weave_w1(1, 1))
+        scatter(2, S)
+        round_plane(1, "scalar")
+        for g in range(2):
+            quantize_w1(1, g, late_w1[g])
+        encode(4)
+        scatter(3, S)
+        round_plane(2, "scalar")
+        v2_sc = sbuf([P, S2], U8, "v2_sc")
+        gather(v2_sc[:], tab2_sc[:], idx2, 0, S2)
+        encode(5)
+        scatter(4, S)
+        round_plane(3, "scalar")
+        weave(0, 0, "scalar")
+        encode(6)
+        scatter(5, S)
+        weave(0, 1, "scalar")
+        weave(0, 2, "scalar")
+        encode(7)
+        scatter(6, S)
+        weave(0, 3, "scalar")
+        round_plane(4, "scalar")
+        scatter(7, S)
+        round_plane(5, "scalar")
+        round_plane(6, "scalar")
+
+        round_plane(7, "vector")
+        for c in range(SCALAR_CHUNKS):
+            weave(1, c, "scalar")
+        v2 = sbuf([P, 2, S2], U32, "v2", "tanh_a")
+        for a in range(2):
+            gather(v2[:, a, :], tab2[a][:].bitcast(U32), idx2, 0, S2)
+        codes0 = sbuf([P, T2], U32, "page_codes_0", "wgs_3")
+        for c in range(CHUNKS):
+            if c >= SCALAR_CHUNKS:
+                weave(1, c, "vector")
+            quantize_page(0, c, codes0[:, c * BANK:(c + 1) * BANK])
+            codes1 = sbuf([P, BANK], U32, "page_codes_1_%d" % c)
+            quantize_page(1, c, codes1[:])
+
+        e = {}
+
+        def score(n):
+            e[n] = sbuf([P, T2], F32, "e_%d" % n, "page", 5)
+            ns = slice(n * P, (n + 1) * P)
+            for c in range(CHUNKS):
+                bank = psum.tile([P, BANK], F32, name="bank", tag="bank_%d" % (CHUNKS * (n % 2) + c))
+                for a in range(2):
+                    nc.tensor.matmul_mx(
+                        out=bank[:], lhsT=v2[:, a, ns].bitcast(FP8X4), lhsT_scale=v2_sc[4 * a:P, ns],
+                        rhs=codes[(a, c)].bitcast(FP8X4), rhs_scale=scales[(a, c)][:],
+                        start=(a == 0), stop=(a == 1),
+                    )
+                copy_on("vector" if (n, c) in VCOPY else "scalar", e[n][:, c * BANK:(c + 1) * BANK], bank[:])
+
+        def finish(n):
+            for lo in range(0, P_OUT, BANK):
+                picked = sbuf([P, BANK], F32, "picked", "picked", 3)
+                gather(picked[:], e[n][:], idx4, lo, lo + BANK)
+                result = sbuf([P, BANK], F32, "result", "woven_%d" % ((2 * n + lo // BANK) % 4))
+                nc.scalar.activation(result[:], picked[:], ACT.Sigmoid, bias=prior_sb[:, n:n + 1])
+                nc.sync.dma_start(out[n * P:(n + 1) * P, lo:lo + BANK], result[:])
+
+        score(0)
+        for n in range(S2 // P):
+            if n + 1 < S2 // P:
+                score(n + 1)
+            finish(n)

@@ -25,7 +25,7 @@ CHUNKS = T2 // BANK
 PLANES = H // P
 SCALAR_CHUNKS = 2
 VCOPY = ()
-TANH_TAG = ["tanh_a", "tanh_b", "tanh_c", "tanh_a", "tanh_b", "tanh_a", "tanh_b", "tanh_a"]
+TANH_TAG = ["tanh_a", "tanh_b", "tanh_c", "tanh_d", "tanh_b", "tanh_e", "tanh_d", "tanh_a"]
 
 
 def tile_list_opening_explorer_scores_kernel(
@@ -63,20 +63,20 @@ def tile_list_opening_explorer_scores_kernel(
             nc.sync.dma_start(t[:], rows[:, i, :])
             return t
 
-        def load_wgs(i):
-            t = sbuf([P, S], F32, "wgs_%d" % i)
+        def load_wgs(i, queue=nc.sync, tag=None):
+            t = sbuf([P, S], F32, "wgs_%d" % i, tag)
             rows = wgs.rearrange("(q i) j -> q i j", i=PACK)[:, i, :]
             for quad in (0, 2, 1, 3):
-                nc.sync.dma_start(t[32 * quad:32 * quad + 32, :], rows)
+                queue.dma_start(t[32 * quad:32 * quad + 32, :], rows)
             return t
 
-        def scale_tile(width, name):
+        def scale_tile(width, name, engine=nc.vector):
             t = sbuf([P, width], U8, name)
-            nc.vector.memset(t[:].bitcast(I32), 0)
+            engine.memset(t[:].bitcast(I32), 0)
             return t
 
-        def load_scales(t, scales, first, count, row, quad):
-            nc.sync.dma_start(
+        def load_scales(t, scales, first, count, row, quad, queue=nc.sync):
+            queue.dma_start(
                 t[32 * quad + row:32 * quad + row + 4 * count, :].bitcast(I32),
                 scales[first:first + count, 4 * quad:4 * quad + 4, :].bitcast(I32),
             )
@@ -84,19 +84,18 @@ def tile_list_opening_explorer_scores_kernel(
         def gather(dst, window, offsets, lo, hi):
             nc.vector.tensor_copy(dst, window.indirect(offsets[:, lo // GROUP:hi // GROUP]))
 
-        tab_sc = scale_tile(T, "tab_sc")
+        tab_sc = scale_tile(T, "tab_sc", nc.gpsimd)
         w4_sc_raw = scale_tile(H, "w4_sc_raw")
         tab2_sc = scale_tile(T, "tab2_sc")
 
         idx = load_list(offs, "idx")
         tab = {2: load_words(tab_words, 2, "tab_2")}
         for quad in range(4):
-            load_scales(tab_sc, tab_scales, 0, 2, 4, quad)
+            load_scales(tab_sc, tab_scales, 0, 2, 4, quad, nc.gpsimd)
         w4_raw = sbuf([P, 2 * H], U8, "w4_raw")
         nc.sync.dma_start(w4_raw[:].bitcast(I32), w4_words[0].bitcast(I32))
-        load_scales(tab_sc, tab_scales, 2, 1, 0, 0)
         tab[0] = load_words(tab_words, 0, "tab_0")
-        for quad in range(1, 4):
+        for quad in range(4):
             load_scales(tab_sc, tab_scales, 2, 1, 0, quad)
         w1_raw = {(0, 0): load_w1(0, 0)}
         for quad in range(4):
@@ -106,6 +105,11 @@ def tile_list_opening_explorer_scores_kernel(
         gain_sb = sbuf([P, 2, PACK], F32, "gain_sb")
         nc.sync.dma_start(gain_sb[:], gain.rearrange("(a p i) -> p a i", p=P, i=PACK))
         idx3 = load_list(offs3, "idx3")
+        w4 = sbuf([P, 2 * H], U8, "w4")
+        nc.vector.tensor_copy(
+            w4[:].bitcast(U16).rearrange("p (a i m) -> p a m i", a=2, i=PACK),
+            w4_raw[:].bitcast(U16).rearrange("p (a m i) -> p a m i", a=2, i=PACK),
+        )
         wgs_sb = [load_wgs(0)]
         page = [load_page(0)]
         wgs_sb.append(load_wgs(1))
@@ -127,11 +131,6 @@ def tile_list_opening_explorer_scores_kernel(
         for k in range(5, PLANES):
             page.append(load_page(k))
 
-        w4 = sbuf([P, 2 * H], U8, "w4")
-        nc.vector.tensor_copy(
-            w4[:].bitcast(U16).rearrange("p (a i m) -> p a m i", a=2, i=PACK),
-            w4_raw[:].bitcast(U16).rearrange("p (a m i) -> p a m i", a=2, i=PACK),
-        )
         v = {a: sbuf([P, S], U32, "v_%d" % a) for a in range(3)}
         v_sc = sbuf([P, S], U8, "v_sc")
         w1_codes, w1_sc = {}, {}
@@ -173,16 +172,16 @@ def tile_list_opening_explorer_scores_kernel(
             for lo in range(0, S, BANK):
                 js = slice(lo, lo + BANK)
                 bank = psum.tile([P, BANK], F32, name="bank", tag="bank_%d" % (2 * (k % 2) + (lo // BANK if k else 0)))
-                nc.tensor.matmul_mx(
-                    out=bank[:], lhsT=w4[:, 2 * col:2 * (col + P)].bitcast(FP4X4), lhsT_scale=w4_sc[:, col:col + P],
-                    rhs=v[2][:, js].bitcast(FP8X4), rhs_scale=v_sc[:, js], start=True, stop=False,
-                )
-                for g in range(2):
+                for g in (0, 2, 1):
+                    if g == 2:
+                        lhs, lhs_sc, row = w4[:, 2 * col:2 * (col + P)].bitcast(FP4X4), w4_sc[:, col:col + P], 0
+                    else:
+                        lhs = w1_codes[(a, g)][:, i * P:(i + 1) * P].bitcast(FP8X4)
+                        lhs_sc, row = w1_sc[(a, g)][:, i * P:(i + 1) * P], 4 * (g + 1)
                     nc.tensor.matmul_mx(
-                        out=bank[:], lhsT=w1_codes[(a, g)][:, i * P:(i + 1) * P].bitcast(FP8X4),
-                        lhsT_scale=w1_sc[(a, g)][:, i * P:(i + 1) * P],
-                        rhs=v[g][:, js].bitcast(FP8X4), rhs_scale=v_sc[4 * (g + 1):P, js],
-                        start=False, stop=(g == 1),
+                        out=bank[:], lhsT=lhs, lhsT_scale=lhs_sc,
+                        rhs=v[g][:, js].bitcast(FP8X4), rhs_scale=v_sc[row:P, js],
+                        start=(g == 0), stop=(g == 1),
                     )
                 if k == 0:
                     raw = sbuf([P, BANK], F32, "tanh_raw", TANH_TAG[1 + lo // BANK])
@@ -220,8 +219,8 @@ def tile_list_opening_explorer_scores_kernel(
             woven[(a, c)] = sbuf([P, PACK * BANK], BF16, "woven_%d_%d" % (a, c), "woven_%d" % (c if a == 0 else 4 + c % SCALAR_CHUNKS))
             copy_on(
                 engine,
-                woven[(a, c)][:].rearrange("p (t u i) -> p t i u", u=4, i=PACK),
-                rounded[(a, c)][:].rearrange("p i (t u) -> p t i u", u=4),
+                woven[(a, c)][:].rearrange("p (t i) -> p t i", i=PACK),
+                rounded[(a, c)][:].rearrange("p i t -> p t i"),
             )
 
         def quantize_page(a, c, dst):

@@ -1,6 +1,7 @@
 from contextlib import ExitStack
 
 import concourse.mybir as mybir
+from concourse.masks import make_identity
 
 K1, K2, T, S, H, T2, S2, P_OUT = 1024, 512, 2048, 1024, 1024, 2048, 512, 1024
 FLOPS = 2 * (K1 + K2) * H * S + 2 * H * S2 * T2
@@ -24,8 +25,10 @@ GROUP = 16
 CHUNKS = T2 // BANK
 PLANES = H // P
 SCALAR_CHUNKS = 2
-VCOPY = ()
-TANH_TAG = ["tanh_a", "tanh_b", "tanh_c", "tanh_d", "tanh_b", "tanh_e", "tanh_d", "tanh_a"]
+VCOPY = ((2, 0), (2, 1))
+FACTOR_TAG = ["factor_%d" % (k % 3) for k in range(8)]
+LAST_EDGES = [0, 512, 768, 1024]
+TANH_TAG = ["tanh_%d" % b for b in (0, 1, 2, 3, 4, 0, 1, 3)]
 
 
 def tile_list_opening_explorer_scores_kernel(
@@ -45,13 +48,13 @@ def tile_list_opening_explorer_scores_kernel(
             nc.sync.dma_start(t[:], src)
             return t
 
-        def load_words(words, a, name):
-            t = sbuf([P, T], I32, name, "slab", 6)
+        def load_words(words, a, name, tag="slab", bufs=5):
+            t = sbuf([P, T], I32, name, tag, bufs)
             nc.sync.dma_start(t[:], words[a].rearrange("p t i -> p (t i)").bitcast(I32))
             return t
 
         def load_w1(a, g):
-            t = sbuf([P, PACK, K_PASS], F32, "w1_raw_%d_%d" % (a, g), "slab", 6)
+            t = sbuf([P, PACK, K_PASS], F32, "w1_raw_%d_%d" % (a, g), "slab", 5)
             rows = w1[g * K_PASS:(g + 1) * K_PASS, a * K_PASS:(a + 1) * K_PASS]
             nc.sync.dma_start(t[:], rows.rearrange("(p j) c -> p j c", j=PACK))
             return t
@@ -63,12 +66,6 @@ def tile_list_opening_explorer_scores_kernel(
             nc.sync.dma_start(t[:], rows[:, i, :])
             return t
 
-        def load_wgs(i, queue=nc.sync, tag=None):
-            t = sbuf([P, S], F32, "wgs_%d" % i, tag)
-            rows = wgs.rearrange("(q i) j -> q i j", i=PACK)[:, i, :]
-            for quad in (0, 2, 1, 3):
-                queue.dma_start(t[32 * quad:32 * quad + 32, :], rows)
-            return t
 
         def scale_tile(width, name, engine=nc.vector):
             t = sbuf([P, width], U8, name)
@@ -92,43 +89,42 @@ def tile_list_opening_explorer_scores_kernel(
         tab = {2: load_words(tab_words, 2, "tab_2")}
         for quad in range(4):
             load_scales(tab_sc, tab_scales, 0, 2, 4, quad, nc.gpsimd)
+        identity = sbuf([P, P], F32, "identity")
+        make_identity(nc, identity[:])
         w4_raw = sbuf([P, 2 * H], U8, "w4_raw")
         nc.sync.dma_start(w4_raw[:].bitcast(I32), w4_words[0].bitcast(I32))
+        wgs_sb = sbuf([P, S], F32, "wgs_sb")
+        nc.sync.dma_start(wgs_sb[:], wgs)
         tab[0] = load_words(tab_words, 0, "tab_0")
         for quad in range(4):
             load_scales(tab_sc, tab_scales, 2, 1, 0, quad)
         w1_raw = {(0, 0): load_w1(0, 0)}
         for quad in range(4):
             load_scales(w4_sc_raw, w4_scales, 0, 1, 0, quad)
-        w1_raw[(0, 1)] = load_w1(0, 1)
-        tab[1] = load_words(tab_words, 1, "tab_1")
         gain_sb = sbuf([P, 2, PACK], F32, "gain_sb")
-        nc.sync.dma_start(gain_sb[:], gain.rearrange("(a p i) -> p a i", p=P, i=PACK))
+        nc.scalar.dma_start(gain_sb[:], gain.rearrange("(a p i) -> p a i", p=P, i=PACK))
+        w1_raw[(0, 1)] = load_w1(0, 1)
+        tab[1] = load_words(tab_words, 1, "tab_1", "tab_1", 1)
         idx3 = load_list(offs3, "idx3")
         w4 = sbuf([P, 2 * H], U8, "w4")
         nc.vector.tensor_copy(
-            w4[:].bitcast(U16).rearrange("p (a i m) -> p a m i", a=2, i=PACK),
-            w4_raw[:].bitcast(U16).rearrange("p (a m i) -> p a m i", a=2, i=PACK),
+            w4[:].bitcast(U16).rearrange("p (a i m) -> p a i m", a=2, i=PACK),
+            w4_raw[:].bitcast(U16).rearrange("p (a m i) -> p a i m", a=2, i=PACK),
         )
-        wgs_sb = [load_wgs(0)]
         page = [load_page(0)]
-        wgs_sb.append(load_wgs(1))
         w1_raw[(1, 0)] = load_w1(1, 0)
         page.append(load_page(1))
         w1_raw[(1, 1)] = load_w1(1, 1)
-        for i in (2, 3):
-            wgs_sb.append(load_wgs(i))
-            page.append(load_page(i))
+        page.append(load_page(2))
         idx2 = load_list(offs2, "idx2")
         for quad in range(4):
             load_scales(tab2_sc, tab2_scales, 0, 2, 0, quad)
-        page.append(load_page(4))
         idx4 = load_list(offs4, "idx4")
         prior_sb = sbuf([P, S2 // P], F32, "prior_sb")
         with nc.allow_non_contiguous_dma(reason="one prior value for each partition"):
             nc.sync.dma_start(prior_sb[:], prior.rearrange("(n p) -> p n", p=P))
         tab2 = [load_words(tab2_words, a, "tab2_%d" % a) for a in range(2)]
-        for k in range(5, PLANES):
+        for k in range(3, PLANES):
             page.append(load_page(k))
 
         v = {a: sbuf([P, S], U32, "v_%d" % a) for a in range(3)}
@@ -136,7 +132,7 @@ def tile_list_opening_explorer_scores_kernel(
         w1_codes, w1_sc = {}, {}
 
         def weave_w1(a, g):
-            t = sbuf([P, PACK * K_PASS], BF16, "w1_b_%d_%d" % (a, g), "woven_%d" % (2 * a + g))
+            t = sbuf([P, PACK * K_PASS], BF16, "w1_b_%d_%d" % (a, g), "spread_1" if (a, g) == (0, 1) else "woven_%d" % (2 * a + g))
             nc.scalar.copy(
                 t[:].rearrange("p (i m j) -> p m j i", i=PACK, j=PACK),
                 w1_raw[(a, g)][:].rearrange("p j (m i) -> p m j i", i=PACK),
@@ -145,33 +141,59 @@ def tile_list_opening_explorer_scores_kernel(
 
         def quantize_w1(a, g, woven):
             if g == 0:
-                w1_codes[a] = sbuf([P, 2, K_PASS], U32, "w1_codes_%d" % a, "tanh_c" if a else None)
+                w1_codes[a] = sbuf([P, 2, K_PASS], U32, "w1_codes_%d" % a, TANH_TAG[2] if a else None)
             w1_codes[(a, g)] = w1_codes[a][:, g, :]
             w1_sc[(a, g)] = sbuf([P, K_PASS], U8, "w1_sc_%d_%d" % (a, g))
             nc.vector.quantize_mx(out=w1_codes[(a, g)].bitcast(FP8X4), scales=w1_sc[(a, g)][:], in_=woven[:])
 
+        def turn(src, first_bank):
+            banks = []
+            for b in range(2):
+                bank = psum.tile([P, BANK], F32, name="bank", tag="bank_%d" % (first_bank + b))
+                for c in range(BANK // P):
+                    col = b * BANK + c * P
+                    nc.tensor.transpose(bank[:, c * P:(c + 1) * P], src[:, col:col + P], identity[:])
+                banks.append(bank)
+            return banks
+
+        wgs_t = turn(wgs_sb, 4)
+        spread = {}
+
+        def spread_plane(i, dst):
+            spread[i] = dst
+            for b in range(2):
+                rows = wgs_t[b][:].rearrange("p (c q i) -> p c q i", q=32, i=PACK)[:, :, :, i]
+                nc.scalar.copy(
+                    dst[:, b * BANK:(b + 1) * BANK].rearrange("p (c g q) -> p c g q", g=4, q=32),
+                    rows.unsqueeze(2).to_broadcast([P, BANK // P, 4, 32]),
+                )
+
+        spread_plane(0, sbuf([P, S], F32, "spread_0")[:])
         gather(v[2][:], tab[2][:].bitcast(U32), idx, 0, S)
         gather(v[0][:], tab[0][:].bitcast(U32), idx, 0, S)
         gather(v_sc[:], tab_sc[:], idx, 0, S)
         quantize_w1(0, 0, weave_w1(0, 0))
         w4_sc = sbuf([P, H], U8, "w4_sc")
         nc.vector.tensor_copy(
-            w4_sc[:].rearrange("p (a i m) -> p a m i", a=2, i=PACK),
-            w4_sc_raw[:].rearrange("p (a m i) -> p a m i", a=2, i=PACK),
+            w4_sc[:].rearrange("p (a i m) -> p a i m", a=2, i=PACK),
+            w4_sc_raw[:].rearrange("p (a m i) -> p a i m", a=2, i=PACK),
         )
         quantize_w1(0, 1, weave_w1(0, 1))
         for lo in range(0, S, BANK):
             gather(v[1][:, lo:lo + BANK], tab[1][:].bitcast(U32), idx, lo, lo + BANK)
 
-        tanh_sb = {}
+        tanh_sb, factor = {}, {}
 
-        def encode(k, step=S):
+        def encode(k):
             a, i = divmod(k, PACK)
             tanh_sb[k] = sbuf([P, S], F32, "tanh_%d" % k, TANH_TAG[k])
+            factor[k] = sbuf([P, S], F32, "factor_%d" % k, FACTOR_TAG[k])
+            for b, bank in enumerate(turn(spread[i], 6)):
+                nc.scalar.activation(factor[k][:, b * BANK:(b + 1) * BANK], bank[:], ACT.Copy, scale=gain_sb[:, a, i:i + 1])
             col = a * K_PASS + i * P
             for lo in range(0, S, BANK):
                 js = slice(lo, lo + BANK)
-                bank = psum.tile([P, BANK], F32, name="bank", tag="bank_%d" % (2 * (k % 2) + (lo // BANK if k else 0)))
+                bank = psum.tile([P, BANK], F32, name="bank", tag="bank_%d" % (2 * (k % 2) + lo // BANK))
                 for g in (0, 2, 1):
                     if g == 2:
                         lhs, lhs_sc, row = w4[:, 2 * col:2 * (col + P)].bitcast(FP4X4), w4_sc[:, col:col + P], 0
@@ -183,21 +205,13 @@ def tile_list_opening_explorer_scores_kernel(
                         rhs=v[g][:, js].bitcast(FP8X4), rhs_scale=v_sc[row:P, js],
                         start=(g == 0), stop=(g == 1),
                     )
-                if k == 0:
-                    raw = sbuf([P, BANK], F32, "tanh_raw", TANH_TAG[1 + lo // BANK])
-                    nc.scalar.activation(raw[:], bank[:], ACT.Tanh)
-                    nc.scalar.activation(tanh_sb[k][:, js], raw[:], ACT.Copy, scale=gain_sb[:, a, i:i + 1])
-                    continue
                 nc.scalar.activation(tanh_sb[k][:, js], bank[:], ACT.Tanh)
-                if (lo + BANK) % step == 0:
-                    part = tanh_sb[k][:, lo + BANK - step:lo + BANK]
-                    nc.scalar.activation(part, part, ACT.Copy, scale=gain_sb[:, a, i:i + 1])
 
         def scatter(k, step):
             for lo in range(0, S, step):
                 nc.vector.tensor_tensor(
                     page[k][:].indirect(idx3[:, lo // GROUP:(lo + step) // GROUP]),
-                    tanh_sb[k][:, lo:lo + step], wgs_sb[k % PACK][:, lo:lo + step], MULT,
+                    tanh_sb[k][:, lo:lo + step], factor[k][:, lo:lo + step], MULT,
                 )
 
         rounded, woven, codes, scales = {}, {}, {}, {}
@@ -228,15 +242,18 @@ def tile_list_opening_explorer_scores_kernel(
             scales[(a, c)] = sbuf([P, BANK], U8, "page_sc_%d_%d" % (a, c))
             nc.vector.quantize_mx(out=dst.bitcast(FP8X4), scales=scales[(a, c)][:], in_=woven[(a, c)][:])
 
-        encode(0, BANK)
+        encode(0)
+        spread_plane(1, sbuf([P, S], F32, "spread_1")[:])
         encode(1)
+        late_spread = sbuf([P, 2, S], F32, "spread_23", "tab_1")
+        spread_plane(2, late_spread[:, 0, :])
         encode(2)
         scatter(0, BANK)
+        spread_plane(3, late_spread[:, 1, :])
         encode(3)
-        late_w1 = [weave_w1(1, 0)]
+        late_w1 = [weave_w1(1, g) for g in range(2)]
         scatter(1, S)
         round_plane(0, "scalar")
-        late_w1.append(weave_w1(1, 1))
         scatter(2, S)
         round_plane(1, "scalar")
         for g in range(2):
@@ -265,10 +282,10 @@ def tile_list_opening_explorer_scores_kernel(
         round_plane(7, "vector")
         for c in range(SCALAR_CHUNKS):
             weave(1, c, "scalar")
-        v2 = sbuf([P, 2, S2], U32, "v2", "tanh_a")
+        v2 = sbuf([P, 2, S2], U32, "v2", TANH_TAG[7])
         for a in range(2):
             gather(v2[:, a, :], tab2[a][:].bitcast(U32), idx2, 0, S2)
-        codes0 = sbuf([P, T2], U32, "page_codes_0", "wgs_3")
+        codes0 = sbuf([P, T2], U32, "page_codes_0", FACTOR_TAG[7])
         for c in range(CHUNKS):
             if c >= SCALAR_CHUNKS:
                 weave(1, c, "vector")
@@ -292,12 +309,13 @@ def tile_list_opening_explorer_scores_kernel(
                 copy_on("vector" if (n, c) in VCOPY else "scalar", e[n][:, c * BANK:(c + 1) * BANK], bank[:])
 
         def finish(n):
-            for lo in range(0, P_OUT, BANK):
-                picked = sbuf([P, BANK], F32, "picked", "picked", 3)
-                gather(picked[:], e[n][:], idx4, lo, lo + BANK)
-                result = sbuf([P, BANK], F32, "result", "woven_%d" % ((2 * n + lo // BANK) % 4))
+            edges = [0, BANK, P_OUT] if n + 1 < S2 // P else LAST_EDGES
+            for lo, hi in zip(edges, edges[1:]):
+                picked = sbuf([P, hi - lo], F32, "picked", "picked", 3)
+                gather(picked[:], e[n][:], idx4, lo, hi)
+                result = sbuf([P, hi - lo], F32, "result", "result", 4)
                 nc.scalar.activation(result[:], picked[:], ACT.Sigmoid, bias=prior_sb[:, n:n + 1])
-                nc.sync.dma_start(out[n * P:(n + 1) * P, lo:lo + BANK], result[:])
+                nc.sync.dma_start(out[n * P:(n + 1) * P, lo:hi], result[:])
 
         score(0)
         for n in range(S2 // P):

@@ -24,9 +24,10 @@ BANK = 512
 GROUP = 16
 CHUNKS = T2 // BANK
 PLANES = H // P
-SCALAR_CHUNKS = 2
-VCOPY = ((2, 0), (2, 1))
-FACTOR_TAG = ["factor_%d" % (k % 3) for k in range(8)]
+SCALAR_CHUNKS = 3
+VCOPY = ((0, 2), (1, 2))
+FACTOR_TAG = ["factor_%d" % b for b in (0, 1, 2, 3, 4, 0, 1, 2)]
+PICK_TAG = ["tanh_%d" % b for b in (0, 1, 2, 4)]
 LAST_EDGES = [0, 512, 768, 1024]
 TANH_TAG = ["tanh_%d" % b for b in (0, 1, 2, 3, 4, 0, 1, 3)]
 
@@ -48,8 +49,8 @@ def tile_list_opening_explorer_scores_kernel(
             nc.sync.dma_start(t[:], src)
             return t
 
-        def load_words(words, a, name, tag="slab", bufs=5):
-            t = sbuf([P, T], I32, name, tag, bufs)
+        def load_words(words, a, name):
+            t = sbuf([P, T], I32, name, "slab", 5)
             nc.sync.dma_start(t[:], words[a].rearrange("p t i -> p (t i)").bitcast(I32))
             return t
 
@@ -83,14 +84,17 @@ def tile_list_opening_explorer_scores_kernel(
 
         tab_sc = scale_tile(T, "tab_sc", nc.gpsimd)
         w4_sc_raw = scale_tile(H, "w4_sc_raw")
-        tab2_sc = scale_tile(T, "tab2_sc")
+        tab2_sc = scale_tile(T, "tab2_sc", nc.gpsimd)
+
+        identity = sbuf([P, P], F32, "identity")
+        make_identity(nc, identity[:])
 
         idx = load_list(offs, "idx")
         tab = {2: load_words(tab_words, 2, "tab_2")}
         for quad in range(4):
             load_scales(tab_sc, tab_scales, 0, 2, 4, quad, nc.gpsimd)
-        identity = sbuf([P, P], F32, "identity")
-        make_identity(nc, identity[:])
+        for quad in range(4):
+            load_scales(tab2_sc, tab2_scales, 0, 2, 0, quad, nc.gpsimd)
         w4_raw = sbuf([P, 2 * H], U8, "w4_raw")
         nc.sync.dma_start(w4_raw[:].bitcast(I32), w4_words[0].bitcast(I32))
         wgs_sb = sbuf([P, S], F32, "wgs_sb")
@@ -98,13 +102,14 @@ def tile_list_opening_explorer_scores_kernel(
         tab[0] = load_words(tab_words, 0, "tab_0")
         for quad in range(4):
             load_scales(tab_sc, tab_scales, 2, 1, 0, quad)
+        idx2 = load_list(offs2, "idx2")
         w1_raw = {(0, 0): load_w1(0, 0)}
         for quad in range(4):
             load_scales(w4_sc_raw, w4_scales, 0, 1, 0, quad)
         gain_sb = sbuf([P, 2, PACK], F32, "gain_sb")
         nc.scalar.dma_start(gain_sb[:], gain.rearrange("(a p i) -> p a i", p=P, i=PACK))
         w1_raw[(0, 1)] = load_w1(0, 1)
-        tab[1] = load_words(tab_words, 1, "tab_1", "tab_1", 1)
+        tab[1] = load_words(tab_words, 1, "tab_1")
         idx3 = load_list(offs3, "idx3")
         w4 = sbuf([P, 2 * H], U8, "w4")
         nc.vector.tensor_copy(
@@ -116,9 +121,6 @@ def tile_list_opening_explorer_scores_kernel(
         page.append(load_page(1))
         w1_raw[(1, 1)] = load_w1(1, 1)
         page.append(load_page(2))
-        idx2 = load_list(offs2, "idx2")
-        for quad in range(4):
-            load_scales(tab2_sc, tab2_scales, 0, 2, 0, quad)
         idx4 = load_list(offs4, "idx4")
         prior_sb = sbuf([P, S2 // P], F32, "prior_sb")
         with nc.allow_non_contiguous_dma(reason="one prior value for each partition"):
@@ -131,20 +133,25 @@ def tile_list_opening_explorer_scores_kernel(
         v_sc = sbuf([P, S], U8, "v_sc")
         w1_codes, w1_sc = {}, {}
 
-        def weave_w1(a, g):
-            t = sbuf([P, PACK * K_PASS], BF16, "w1_b_%d_%d" % (a, g), "spread_1" if (a, g) == (0, 1) else "woven_%d" % (2 * a + g))
+        def weave_w1(a, g, tag, first=0, last=PACK):
+            t = sbuf([P, last - first, K_PASS], BF16, "w1_woven", tag)
             nc.scalar.copy(
-                t[:].rearrange("p (i m j) -> p m j i", i=PACK, j=PACK),
-                w1_raw[(a, g)][:].rearrange("p j (m i) -> p m j i", i=PACK),
+                t[:].rearrange("p i (m j) -> p m j i", j=PACK),
+                w1_raw[(a, g)][:].rearrange("p j (m i) -> p m j i", i=PACK)[:, :, :, first:last],
             )
             return t
 
-        def quantize_w1(a, g, woven):
+        def quantize_w1(a, g, woven, first=0):
             if g == 0:
                 w1_codes[a] = sbuf([P, 2, K_PASS], U32, "w1_codes_%d" % a, TANH_TAG[2] if a else None)
-            w1_codes[(a, g)] = w1_codes[a][:, g, :]
-            w1_sc[(a, g)] = sbuf([P, K_PASS], U8, "w1_sc_%d_%d" % (a, g))
-            nc.vector.quantize_mx(out=w1_codes[(a, g)].bitcast(FP8X4), scales=w1_sc[(a, g)][:], in_=woven[:])
+            if first == 0:
+                w1_codes[(a, g)] = w1_codes[a][:, g, :]
+                w1_sc[(a, g)] = sbuf([P, K_PASS], U8, "w1_sc_%d_%d" % (a, g))
+            cols = slice(first * P, (first + woven.shape[1]) * P)
+            nc.vector.quantize_mx(
+                out=w1_codes[(a, g)][:, cols].bitcast(FP8X4), scales=w1_sc[(a, g)][:, cols],
+                in_=woven.rearrange("p i c -> p (i c)"),
+            )
 
         def turn(src, first_bank):
             banks = []
@@ -172,28 +179,38 @@ def tile_list_opening_explorer_scores_kernel(
         gather(v[2][:], tab[2][:].bitcast(U32), idx, 0, S)
         gather(v[0][:], tab[0][:].bitcast(U32), idx, 0, S)
         gather(v_sc[:], tab_sc[:], idx, 0, S)
-        quantize_w1(0, 0, weave_w1(0, 0))
+        v2_sc = sbuf([P, S2], U8, "v2_sc")
+        gather(v2_sc[:], tab2_sc[:], idx2, 0, S2)
+        quantize_w1(0, 0, weave_w1(0, 0, "woven_0")[:])
         w4_sc = sbuf([P, H], U8, "w4_sc")
         nc.vector.tensor_copy(
             w4_sc[:].rearrange("p (a i m) -> p a i m", a=2, i=PACK),
             w4_sc_raw[:].rearrange("p (a m i) -> p a i m", a=2, i=PACK),
         )
-        quantize_w1(0, 1, weave_w1(0, 1))
+        quantize_w1(0, 1, weave_w1(0, 1, "spread_1", 0, 1)[:])
+        rest = weave_w1(0, 1, "spread_1", 1, PACK)
         for lo in range(0, S, BANK):
             gather(v[1][:, lo:lo + BANK], tab[1][:].bitcast(U32), idx, lo, lo + BANK)
+        quantize_w1(0, 1, rest[:, 0:1, :], 1)
+        quantize_w1(0, 1, rest[:, 1:3, :], 2)
 
         tanh_sb, factor = {}, {}
+
+        def make_factors(i, passes):
+            banks = turn(spread[i], 6)
+            for a in passes:
+                k = a * PACK + i
+                factor[k] = sbuf([P, S], F32, "factor_%d" % k, FACTOR_TAG[k])
+                for b, bank in enumerate(banks):
+                    nc.scalar.activation(factor[k][:, b * BANK:(b + 1) * BANK], bank[:], ACT.Copy, scale=gain_sb[:, a, i:i + 1])
 
         def encode(k):
             a, i = divmod(k, PACK)
             tanh_sb[k] = sbuf([P, S], F32, "tanh_%d" % k, TANH_TAG[k])
-            factor[k] = sbuf([P, S], F32, "factor_%d" % k, FACTOR_TAG[k])
-            for b, bank in enumerate(turn(spread[i], 6)):
-                nc.scalar.activation(factor[k][:, b * BANK:(b + 1) * BANK], bank[:], ACT.Copy, scale=gain_sb[:, a, i:i + 1])
             col = a * K_PASS + i * P
             for lo in range(0, S, BANK):
                 js = slice(lo, lo + BANK)
-                bank = psum.tile([P, BANK], F32, name="bank", tag="bank_%d" % (2 * (k % 2) + lo // BANK))
+                bank = psum.tile([P, BANK], F32, name="bank", tag="bank_%d" % ((4 if k % 2 and k > 1 else 0) + lo // BANK))
                 for g in (0, 2, 1):
                     if g == 2:
                         lhs, lhs_sc, row = w4[:, 2 * col:2 * (col + P)].bitcast(FP4X4), w4_sc[:, col:col + P], 0
@@ -230,7 +247,7 @@ def tile_list_opening_explorer_scores_kernel(
                 copy_on(engine, rounded[(a, c)][:, i, :], page[k][:, c * BANK:(c + 1) * BANK])
 
         def weave(a, c, engine):
-            woven[(a, c)] = sbuf([P, PACK * BANK], BF16, "woven_%d_%d" % (a, c), "woven_%d" % (c if a == 0 else 4 + c % SCALAR_CHUNKS))
+            woven[(a, c)] = sbuf([P, PACK * BANK], BF16, "woven_%d_%d" % (a, c), "woven_%d" % (c + 4 * a))
             copy_on(
                 engine,
                 woven[(a, c)][:].rearrange("p (t i) -> p t i", i=PACK),
@@ -242,35 +259,40 @@ def tile_list_opening_explorer_scores_kernel(
             scales[(a, c)] = sbuf([P, BANK], U8, "page_sc_%d_%d" % (a, c))
             nc.vector.quantize_mx(out=dst.bitcast(FP8X4), scales=scales[(a, c)][:], in_=woven[(a, c)][:])
 
+        make_factors(0, (0, 1))
         encode(0)
-        spread_plane(1, sbuf([P, S], F32, "spread_1")[:])
+        late_spread = sbuf([P, 3, S], F32, "late_spread", "spread_1")
+        spread_plane(1, late_spread[:, 0, :])
+        make_factors(1, (0,))
         encode(1)
-        late_spread = sbuf([P, 2, S], F32, "spread_23", "tab_1")
-        spread_plane(2, late_spread[:, 0, :])
+        spread_plane(2, late_spread[:, 1, :])
+        make_factors(2, (0,))
         encode(2)
         scatter(0, BANK)
-        spread_plane(3, late_spread[:, 1, :])
+        spread_plane(3, late_spread[:, 2, :])
+        make_factors(3, (0,))
         encode(3)
-        late_w1 = [weave_w1(1, g) for g in range(2)]
+        late_w1 = [weave_w1(1, g, "woven_%d" % (2 + g))[:] for g in range(2)]
         scatter(1, S)
         round_plane(0, "scalar")
         scatter(2, S)
         round_plane(1, "scalar")
         for g in range(2):
             quantize_w1(1, g, late_w1[g])
+        round_plane(2, "scalar")
         encode(4)
         scatter(3, S)
-        round_plane(2, "scalar")
-        v2_sc = sbuf([P, S2], U8, "v2_sc")
-        gather(v2_sc[:], tab2_sc[:], idx2, 0, S2)
+        make_factors(1, (1,))
         encode(5)
         scatter(4, S)
         round_plane(3, "scalar")
         weave(0, 0, "scalar")
+        make_factors(2, (1,))
         encode(6)
         scatter(5, S)
         weave(0, 1, "scalar")
         weave(0, 2, "scalar")
+        make_factors(3, (1,))
         encode(7)
         scatter(6, S)
         weave(0, 3, "scalar")
@@ -290,7 +312,7 @@ def tile_list_opening_explorer_scores_kernel(
             if c >= SCALAR_CHUNKS:
                 weave(1, c, "vector")
             quantize_page(0, c, codes0[:, c * BANK:(c + 1) * BANK])
-            codes1 = sbuf([P, BANK], U32, "page_codes_1_%d" % c)
+            codes1 = sbuf([P, BANK], U32, "page_codes_1_%d" % c, ("v_0", "v_1", "v_2", "wgs_sb")[c])
             quantize_page(1, c, codes1[:])
 
         e = {}
@@ -309,16 +331,14 @@ def tile_list_opening_explorer_scores_kernel(
                 copy_on("vector" if (n, c) in VCOPY else "scalar", e[n][:, c * BANK:(c + 1) * BANK], bank[:])
 
         def finish(n):
+            picked = sbuf([P, P_OUT], F32, "picked_%d" % n, PICK_TAG[n])
             edges = [0, BANK, P_OUT] if n + 1 < S2 // P else LAST_EDGES
             for lo, hi in zip(edges, edges[1:]):
-                picked = sbuf([P, hi - lo], F32, "picked", "picked", 3)
-                gather(picked[:], e[n][:], idx4, lo, hi)
-                result = sbuf([P, hi - lo], F32, "result", "result", 4)
-                nc.scalar.activation(result[:], picked[:], ACT.Sigmoid, bias=prior_sb[:, n:n + 1])
-                nc.sync.dma_start(out[n * P:(n + 1) * P, lo:hi], result[:])
+                gather(picked[:, lo:hi], e[n][:], idx4, lo, hi)
+                nc.scalar.activation(picked[:, lo:hi], picked[:, lo:hi], ACT.Sigmoid, bias=prior_sb[:, n:n + 1])
+                nc.sync.dma_start(out[n * P:(n + 1) * P, lo:hi], picked[:, lo:hi])
 
-        score(0)
         for n in range(S2 // P):
-            if n + 1 < S2 // P:
-                score(n + 1)
+            score(n)
+        for n in range(S2 // P):
             finish(n)

@@ -3,8 +3,10 @@ from contextlib import ExitStack
 import concourse.mybir as mybir
 from concourse.masks import make_identity
 
-K1, K2, T, S, H, T2, S2, P_OUT = 1024, 512, 2048, 1024, 1024, 2048, 512, 1024
-FLOPS = 2 * (K1 + K2) * H * S + 2 * H * S2 * T2
+K1, K2, H = 1024, 512, 1024
+COLUMNS = 2048
+BOARDS, MOVES, PICKS = 1024, 512, 1024
+FLOPS = 2 * (K1 + K2) * H * BOARDS + 2 * H * MOVES * COLUMNS
 
 F32 = mybir.dt.float32
 BF16 = mybir.dt.bfloat16
@@ -18,18 +20,29 @@ ACT = mybir.ActivationFunctionType
 MULT = mybir.AluOpType.mult
 
 P = 128
+QUADRANT = 32
 PACK = 4
 K_PASS = P * PACK
 BANK = 512
 GROUP = 16
-CHUNKS = T2 // BANK
 PLANES = H // P
-SCALAR_CHUNKS = 3
-VCOPY = ((0, 2), (1, 2))
-FACTOR_TAG = ["factor_%d" % b for b in (0, 1, 2, 3, 4, 0, 1, 2)]
-PICK_TAG = ["tanh_%d" % b for b in (0, 1, 2, 4)]
-LAST_EDGES = [0, 512, 768, 1024]
+CHUNKS = COLUMNS // BANK
+MOVE_TILES = MOVES // P
+W4_PASS = K1 // K_PASS
+TAB_SCALE_ROW = {0: 4, 1: 8, W4_PASS: 0}
+
+SLABS = 5
+PAGE_BUFS = 5
 TANH_TAG = ["tanh_%d" % b for b in (0, 1, 2, 3, 4, 0, 1, 3)]
+PICK_TAG = ["tanh_%d" % b for b in (0, 1, 2, 4)]
+FACTOR_TAG = ["factor_%d" % (k % 5) for k in range(PLANES)]
+LAST_CODES_TAG = ("v_0", "v_1", "v_2", "wgs_sb")
+H_BANKS, WGS_BANKS, FACTOR_BANKS = 0, 4, 6
+
+SCALAR_ROUNDS = 2
+SCALAR_WEAVES = 3
+VECTOR_BANKS = ((0, SCALAR_WEAVES - 1), (1, SCALAR_WEAVES - 1))
+LAST_EDGES = [0, 512, 768, 1024]
 
 
 def tile_list_opening_explorer_scores_kernel(
@@ -44,68 +57,71 @@ def tile_list_opening_explorer_scores_kernel(
         def sbuf(shape, dtype, name, tag=None, bufs=1):
             return keep.tile(shape, dtype, name=name, tag=tag or name, bufs=bufs, align_bytes=64)
 
+        def psum_bank(number):
+            return psum.tile([P, BANK], F32, name="bank", tag="bank_%d" % number)
+
+        def copy_on(on_scalar, dst, src):
+            if on_scalar:
+                nc.scalar.copy(dst, src)
+            else:
+                nc.vector.tensor_copy(dst, src)
+
         def load_list(src, name):
-            t = keep.tile(list(src.shape), U16, name=name, tag=name)
-            nc.sync.dma_start(t[:], src)
-            return t
+            offsets = keep.tile(list(src.shape), U16, name=name, tag=name)
+            nc.sync.dma_start(offsets[:], src)
+            return offsets
 
         def load_words(words, a, name):
-            t = sbuf([P, T], I32, name, "slab", 5)
-            nc.sync.dma_start(t[:], words[a].rearrange("p t i -> p (t i)").bitcast(I32))
-            return t
+            window = sbuf([P, COLUMNS], I32, name, "slab", SLABS)
+            nc.sync.dma_start(window[:], words[a].rearrange("p t i -> p (t i)").bitcast(I32))
+            return window
 
         def load_w1(a, g):
-            t = sbuf([P, PACK, K_PASS], F32, "w1_raw_%d_%d" % (a, g), "slab", 5)
+            raw = sbuf([P, PACK, K_PASS], F32, "w1_raw_%d_%d" % (a, g), "slab", SLABS)
             rows = w1[g * K_PASS:(g + 1) * K_PASS, a * K_PASS:(a + 1) * K_PASS]
-            nc.sync.dma_start(t[:], rows.rearrange("(p j) c -> p j c", j=PACK))
-            return t
+            nc.sync.dma_start(raw[:], rows.rearrange("(p j) c -> p j c", j=PACK))
+            return raw
 
         def load_page(k):
             a, i = divmod(k, PACK)
-            t = sbuf([P, T2], F32, "page_%d" % k, "page", 5)
+            plane = sbuf([P, COLUMNS], F32, "page_%d" % k, "page", PAGE_BUFS)
             rows = page0[a * K_PASS:(a + 1) * K_PASS, :].rearrange("(p i) t -> p i t", i=PACK)
-            nc.sync.dma_start(t[:], rows[:, i, :])
-            return t
+            nc.sync.dma_start(plane[:], rows[:, i, :])
+            return plane
 
+        def scale_tile(width, name):
+            rows = sbuf([P, width], U8, name)
+            nc.vector.memset(rows[:].bitcast(I32), 0)
+            return rows
 
-        def scale_tile(width, name, engine=nc.vector):
-            t = sbuf([P, width], U8, name)
-            engine.memset(t[:].bitcast(I32), 0)
-            return t
-
-        def load_scales(t, scales, first, count, row, quad, queue=nc.sync):
-            queue.dma_start(
-                t[32 * quad + row:32 * quad + row + 4 * count, :].bitcast(I32),
-                scales[first:first + count, 4 * quad:4 * quad + 4, :].bitcast(I32),
-            )
+        def load_scales(queue, dst, scales, first, count, row):
+            for quad in range(P // QUADRANT):
+                base = QUADRANT * quad + row
+                queue.dma_start(
+                    dst[base:base + 4 * count, :].bitcast(I32),
+                    scales[first:first + count, 4 * quad:4 * quad + 4, :].bitcast(I32),
+                )
 
         def gather(dst, window, offsets, lo, hi):
             nc.vector.tensor_copy(dst, window.indirect(offsets[:, lo // GROUP:hi // GROUP]))
 
-        tab_sc = scale_tile(T, "tab_sc", nc.gpsimd)
+        tab_sc = scale_tile(COLUMNS, "tab_sc")
         w4_sc_raw = scale_tile(H, "w4_sc_raw")
-        tab2_sc = scale_tile(T, "tab2_sc", nc.gpsimd)
-
+        tab2_sc = scale_tile(COLUMNS, "tab2_sc")
         identity = sbuf([P, P], F32, "identity")
         make_identity(nc, identity[:])
 
         idx = load_list(offs, "idx")
-        tab = {2: load_words(tab_words, 2, "tab_2")}
-        for quad in range(4):
-            load_scales(tab_sc, tab_scales, 0, 2, 4, quad, nc.gpsimd)
-        for quad in range(4):
-            load_scales(tab2_sc, tab2_scales, 0, 2, 0, quad, nc.gpsimd)
+        tab = {W4_PASS: load_words(tab_words, W4_PASS, "tab_2")}
+        load_scales(nc.gpsimd, tab_sc, tab_scales, 0, 2, TAB_SCALE_ROW[0])
         w4_raw = sbuf([P, 2 * H], U8, "w4_raw")
         nc.sync.dma_start(w4_raw[:].bitcast(I32), w4_words[0].bitcast(I32))
-        wgs_sb = sbuf([P, S], F32, "wgs_sb")
+        wgs_sb = sbuf([P, BOARDS], F32, "wgs_sb")
         nc.sync.dma_start(wgs_sb[:], wgs)
         tab[0] = load_words(tab_words, 0, "tab_0")
-        for quad in range(4):
-            load_scales(tab_sc, tab_scales, 2, 1, 0, quad)
-        idx2 = load_list(offs2, "idx2")
+        load_scales(nc.sync, tab_sc, tab_scales, W4_PASS, 1, TAB_SCALE_ROW[W4_PASS])
         w1_raw = {(0, 0): load_w1(0, 0)}
-        for quad in range(4):
-            load_scales(w4_sc_raw, w4_scales, 0, 1, 0, quad)
+        load_scales(nc.sync, w4_sc_raw, w4_scales, 0, 1, 0)
         gain_sb = sbuf([P, 2, PACK], F32, "gain_sb")
         nc.scalar.dma_start(gain_sb[:], gain.rearrange("(a p i) -> p a i", p=P, i=PACK))
         w1_raw[(0, 1)] = load_w1(0, 1)
@@ -121,111 +137,113 @@ def tile_list_opening_explorer_scores_kernel(
         page.append(load_page(1))
         w1_raw[(1, 1)] = load_w1(1, 1)
         page.append(load_page(2))
+        idx2 = load_list(offs2, "idx2")
+        load_scales(nc.sync, tab2_sc, tab2_scales, 0, 2, 0)
         idx4 = load_list(offs4, "idx4")
-        prior_sb = sbuf([P, S2 // P], F32, "prior_sb")
+        prior_sb = sbuf([P, MOVE_TILES], F32, "prior_sb")
         with nc.allow_non_contiguous_dma(reason="one prior value for each partition"):
             nc.sync.dma_start(prior_sb[:], prior.rearrange("(n p) -> p n", p=P))
         tab2 = [load_words(tab2_words, a, "tab2_%d" % a) for a in range(2)]
         for k in range(3, PLANES):
             page.append(load_page(k))
 
-        v = {a: sbuf([P, S], U32, "v_%d" % a) for a in range(3)}
-        v_sc = sbuf([P, S], U8, "v_sc")
+        v = {g: sbuf([P, BOARDS], U32, "v_%d" % g) for g in range(3)}
+        v_sc = sbuf([P, BOARDS], U8, "v_sc")
         w1_codes, w1_sc = {}, {}
 
         def weave_w1(a, g, tag, first=0, last=PACK):
-            t = sbuf([P, last - first, K_PASS], BF16, "w1_woven", tag)
+            woven_w1 = sbuf([P, last - first, K_PASS], BF16, "w1_woven", tag)
             nc.scalar.copy(
-                t[:].rearrange("p i (m j) -> p m j i", j=PACK),
+                woven_w1[:].rearrange("p i (m j) -> p m j i", j=PACK),
                 w1_raw[(a, g)][:].rearrange("p j (m i) -> p m j i", i=PACK)[:, :, :, first:last],
             )
-            return t
+            return woven_w1[:]
 
-        def quantize_w1(a, g, woven, first=0):
-            if g == 0:
-                w1_codes[a] = sbuf([P, 2, K_PASS], U32, "w1_codes_%d" % a, TANH_TAG[2] if a else None)
+        def quantize_w1(a, g, woven_w1, first=0):
             if first == 0:
-                w1_codes[(a, g)] = w1_codes[a][:, g, :]
                 w1_sc[(a, g)] = sbuf([P, K_PASS], U8, "w1_sc_%d_%d" % (a, g))
-            cols = slice(first * P, (first + woven.shape[1]) * P)
+            cols = slice(first * P, (first + woven_w1.shape[1]) * P)
             nc.vector.quantize_mx(
-                out=w1_codes[(a, g)][:, cols].bitcast(FP8X4), scales=w1_sc[(a, g)][:, cols],
-                in_=woven.rearrange("p i c -> p (i c)"),
+                out=w1_codes[a][:, g, cols].bitcast(FP8X4), scales=w1_sc[(a, g)][:, cols],
+                in_=woven_w1.rearrange("p i c -> p (i c)"),
             )
 
         def turn(src, first_bank):
             banks = []
             for b in range(2):
-                bank = psum.tile([P, BANK], F32, name="bank", tag="bank_%d" % (first_bank + b))
+                bank = psum_bank(first_bank + b)
                 for c in range(BANK // P):
                     col = b * BANK + c * P
                     nc.tensor.transpose(bank[:, c * P:(c + 1) * P], src[:, col:col + P], identity[:])
                 banks.append(bank)
             return banks
 
-        wgs_t = turn(wgs_sb, 4)
+        wgs_turned = turn(wgs_sb, WGS_BANKS)
         spread = {}
 
-        def spread_plane(i, dst):
+        def spread_rows(i, dst):
             spread[i] = dst
             for b in range(2):
-                rows = wgs_t[b][:].rearrange("p (c q i) -> p c q i", q=32, i=PACK)[:, :, :, i]
+                rows = wgs_turned[b][:].rearrange("p (c q i) -> p c q i", q=QUADRANT, i=PACK)[:, :, :, i]
                 nc.scalar.copy(
-                    dst[:, b * BANK:(b + 1) * BANK].rearrange("p (c g q) -> p c g q", g=4, q=32),
-                    rows.unsqueeze(2).to_broadcast([P, BANK // P, 4, 32]),
+                    dst[:, b * BANK:(b + 1) * BANK].rearrange("p (c g q) -> p c g q", g=P // QUADRANT, q=QUADRANT),
+                    rows.unsqueeze(2).to_broadcast([P, BANK // P, P // QUADRANT, QUADRANT]),
                 )
 
-        spread_plane(0, sbuf([P, S], F32, "spread_0")[:])
-        gather(v[2][:], tab[2][:].bitcast(U32), idx, 0, S)
-        gather(v[0][:], tab[0][:].bitcast(U32), idx, 0, S)
-        gather(v_sc[:], tab_sc[:], idx, 0, S)
-        v2_sc = sbuf([P, S2], U8, "v2_sc")
-        gather(v2_sc[:], tab2_sc[:], idx2, 0, S2)
-        quantize_w1(0, 0, weave_w1(0, 0, "woven_0")[:])
+        spread_rows(0, sbuf([P, BOARDS], F32, "spread_0")[:])
+        gather(v[W4_PASS][:], tab[W4_PASS][:].bitcast(U32), idx, 0, BOARDS)
+        gather(v[0][:], tab[0][:].bitcast(U32), idx, 0, BOARDS)
+        gather(v_sc[:], tab_sc[:], idx, 0, BOARDS)
+        first_w1 = weave_w1(0, 0, "woven_0")
+        w1_codes[0] = sbuf([P, 2, K_PASS], U32, "w1_codes_0")
+        quantize_w1(0, 0, first_w1)
         w4_sc = sbuf([P, H], U8, "w4_sc")
         nc.vector.tensor_copy(
             w4_sc[:].rearrange("p (a i m) -> p a i m", a=2, i=PACK),
             w4_sc_raw[:].rearrange("p (a m i) -> p a i m", a=2, i=PACK),
         )
-        quantize_w1(0, 1, weave_w1(0, 1, "spread_1", 0, 1)[:])
-        rest = weave_w1(0, 1, "spread_1", 1, PACK)
-        for lo in range(0, S, BANK):
+        quantize_w1(0, 1, weave_w1(0, 1, "spread_rest", 0, 1))
+        rest_w1 = weave_w1(0, 1, "spread_rest", 1, PACK)
+        for lo in range(0, BOARDS, BANK):
             gather(v[1][:, lo:lo + BANK], tab[1][:].bitcast(U32), idx, lo, lo + BANK)
-        quantize_w1(0, 1, rest[:, 0:1, :], 1)
-        quantize_w1(0, 1, rest[:, 1:3, :], 2)
+        quantize_w1(0, 1, rest_w1[:, 0:1, :], 1)
+        quantize_w1(0, 1, rest_w1[:, 1:3, :], 2)
 
         tanh_sb, factor = {}, {}
 
         def make_factors(i, passes):
-            banks = turn(spread[i], 6)
+            banks = turn(spread[i], FACTOR_BANKS)
             for a in passes:
                 k = a * PACK + i
-                factor[k] = sbuf([P, S], F32, "factor_%d" % k, FACTOR_TAG[k])
+                factor[k] = sbuf([P, BOARDS], F32, "factor_%d" % k, FACTOR_TAG[k])
                 for b, bank in enumerate(banks):
-                    nc.scalar.activation(factor[k][:, b * BANK:(b + 1) * BANK], bank[:], ACT.Copy, scale=gain_sb[:, a, i:i + 1])
+                    nc.scalar.activation(
+                        factor[k][:, b * BANK:(b + 1) * BANK], bank[:], ACT.Copy, scale=gain_sb[:, a, i:i + 1]
+                    )
 
         def encode(k):
             a, i = divmod(k, PACK)
-            tanh_sb[k] = sbuf([P, S], F32, "tanh_%d" % k, TANH_TAG[k])
+            tanh_sb[k] = sbuf([P, BOARDS], F32, "tanh_%d" % k, TANH_TAG[k])
+            plane_cols = slice(i * P, (i + 1) * P)
             col = a * K_PASS + i * P
-            for lo in range(0, S, BANK):
+            first_bank = WGS_BANKS if k % 2 and k > 1 else H_BANKS
+            for lo in range(0, BOARDS, BANK):
                 js = slice(lo, lo + BANK)
-                bank = psum.tile([P, BANK], F32, name="bank", tag="bank_%d" % ((4 if k % 2 and k > 1 else 0) + lo // BANK))
-                for g in (0, 2, 1):
-                    if g == 2:
-                        lhs, lhs_sc, row = w4[:, 2 * col:2 * (col + P)].bitcast(FP4X4), w4_sc[:, col:col + P], 0
+                bank = psum_bank(first_bank + lo // BANK)
+                for g in (0, W4_PASS, 1):
+                    if g == W4_PASS:
+                        lhs, lhs_sc = w4[:, 2 * col:2 * (col + P)].bitcast(FP4X4), w4_sc[:, col:col + P]
                     else:
-                        lhs = w1_codes[(a, g)][:, i * P:(i + 1) * P].bitcast(FP8X4)
-                        lhs_sc, row = w1_sc[(a, g)][:, i * P:(i + 1) * P], 4 * (g + 1)
+                        lhs, lhs_sc = w1_codes[a][:, g, plane_cols].bitcast(FP8X4), w1_sc[(a, g)][:, plane_cols]
                     nc.tensor.matmul_mx(
                         out=bank[:], lhsT=lhs, lhsT_scale=lhs_sc,
-                        rhs=v[g][:, js].bitcast(FP8X4), rhs_scale=v_sc[row:P, js],
+                        rhs=v[g][:, js].bitcast(FP8X4), rhs_scale=v_sc[TAB_SCALE_ROW[g]:P, js],
                         start=(g == 0), stop=(g == 1),
                     )
                 nc.scalar.activation(tanh_sb[k][:, js], bank[:], ACT.Tanh)
 
-        def scatter(k, step):
-            for lo in range(0, S, step):
+        def scatter(k, step=BOARDS):
+            for lo in range(0, BOARDS, step):
                 nc.vector.tensor_tensor(
                     page[k][:].indirect(idx3[:, lo // GROUP:(lo + step) // GROUP]),
                     tanh_sb[k][:, lo:lo + step], factor[k][:, lo:lo + step], MULT,
@@ -233,23 +251,17 @@ def tile_list_opening_explorer_scores_kernel(
 
         rounded, woven, codes, scales = {}, {}, {}, {}
 
-        def copy_on(engine, dst, src):
-            if engine == "scalar":
-                nc.scalar.copy(dst, src)
-            else:
-                nc.vector.tensor_copy(dst, src)
-
-        def round_plane(k, engine):
+        def round_plane(k, scalar_chunks=CHUNKS):
             a, i = divmod(k, PACK)
             for c in range(CHUNKS):
                 if i == 0:
                     rounded[(a, c)] = sbuf([P, PACK, BANK], BF16, "rounded_%d_%d" % (a, c), "rounded_%d" % c)
-                copy_on(engine, rounded[(a, c)][:, i, :], page[k][:, c * BANK:(c + 1) * BANK])
+                copy_on(c < scalar_chunks, rounded[(a, c)][:, i, :], page[k][:, c * BANK:(c + 1) * BANK])
 
-        def weave(a, c, engine):
-            woven[(a, c)] = sbuf([P, PACK * BANK], BF16, "woven_%d_%d" % (a, c), "woven_%d" % (c + 4 * a))
+        def weave(a, c, on_scalar=True):
+            woven[(a, c)] = sbuf([P, PACK * BANK], BF16, "woven_%d_%d" % (a, c), "woven_%d" % (CHUNKS * a + c))
             copy_on(
-                engine,
+                on_scalar,
                 woven[(a, c)][:].rearrange("p (t i) -> p t i", i=PACK),
                 rounded[(a, c)][:].rearrange("p i t -> p t i"),
             )
@@ -261,84 +273,77 @@ def tile_list_opening_explorer_scores_kernel(
 
         make_factors(0, (0, 1))
         encode(0)
-        late_spread = sbuf([P, 3, S], F32, "late_spread", "spread_1")
-        spread_plane(1, late_spread[:, 0, :])
-        make_factors(1, (0,))
-        encode(1)
-        spread_plane(2, late_spread[:, 1, :])
-        make_factors(2, (0,))
-        encode(2)
+        spread_rest = sbuf([P, PACK - 1, BOARDS], F32, "spread_rest")
+        for i in (1, 2):
+            spread_rows(i, spread_rest[:, i - 1, :])
+            make_factors(i, (0,))
+            encode(i)
         scatter(0, BANK)
-        spread_plane(3, late_spread[:, 2, :])
+        spread_rows(3, spread_rest[:, 2, :])
         make_factors(3, (0,))
         encode(3)
-        late_w1 = [weave_w1(1, g, "woven_%d" % (2 + g))[:] for g in range(2)]
-        scatter(1, S)
-        round_plane(0, "scalar")
-        scatter(2, S)
-        round_plane(1, "scalar")
+        late_w1 = [weave_w1(1, g, "woven_%d" % (2 + g)) for g in range(2)]
+        for k in (1, 2):
+            scatter(k)
+            round_plane(k - 1)
+        w1_codes[1] = sbuf([P, 2, K_PASS], U32, "w1_codes_1", TANH_TAG[2])
         for g in range(2):
             quantize_w1(1, g, late_w1[g])
-        round_plane(2, "scalar")
+        v2_sc = sbuf([P, MOVES], U8, "v2_sc")
+        gather(v2_sc[:], tab2_sc[:], idx2, 0, MOVES)
+        round_plane(2)
         encode(4)
-        scatter(3, S)
+        scatter(3)
         make_factors(1, (1,))
         encode(5)
-        scatter(4, S)
-        round_plane(3, "scalar")
-        weave(0, 0, "scalar")
+        scatter(4)
+        round_plane(3)
+        weave(0, 0)
         make_factors(2, (1,))
         encode(6)
-        scatter(5, S)
-        weave(0, 1, "scalar")
-        weave(0, 2, "scalar")
+        scatter(5)
+        weave(0, 1)
+        weave(0, 2)
         make_factors(3, (1,))
         encode(7)
-        scatter(6, S)
-        weave(0, 3, "scalar")
-        round_plane(4, "scalar")
-        scatter(7, S)
-        round_plane(5, "scalar")
-        round_plane(6, "scalar")
+        scatter(6)
+        weave(0, 3)
+        round_plane(4)
+        scatter(7)
+        round_plane(5)
+        round_plane(6)
 
-        round_plane(7, "vector")
-        for c in range(SCALAR_CHUNKS):
-            weave(1, c, "scalar")
-        v2 = sbuf([P, 2, S2], U32, "v2", TANH_TAG[7])
+        round_plane(7, SCALAR_ROUNDS)
+        for c in range(SCALAR_WEAVES):
+            weave(1, c)
+        v2 = sbuf([P, 2, MOVES], U32, "v2", TANH_TAG[7])
         for a in range(2):
-            gather(v2[:, a, :], tab2[a][:].bitcast(U32), idx2, 0, S2)
-        codes0 = sbuf([P, T2], U32, "page_codes_0", FACTOR_TAG[7])
+            gather(v2[:, a, :], tab2[a][:].bitcast(U32), idx2, 0, MOVES)
+        first_codes = sbuf([P, COLUMNS], U32, "page_codes_0", FACTOR_TAG[7])
         for c in range(CHUNKS):
-            if c >= SCALAR_CHUNKS:
-                weave(1, c, "vector")
-            quantize_page(0, c, codes0[:, c * BANK:(c + 1) * BANK])
-            codes1 = sbuf([P, BANK], U32, "page_codes_1_%d" % c, ("v_0", "v_1", "v_2", "wgs_sb")[c])
-            quantize_page(1, c, codes1[:])
+            if c >= SCALAR_WEAVES:
+                weave(1, c, on_scalar=False)
+            quantize_page(0, c, first_codes[:, c * BANK:(c + 1) * BANK])
+            quantize_page(1, c, sbuf([P, BANK], U32, "page_codes_1_%d" % c, LAST_CODES_TAG[c])[:])
 
-        e = {}
-
-        def score(n):
-            e[n] = sbuf([P, T2], F32, "e_%d" % n, "page", 5)
-            ns = slice(n * P, (n + 1) * P)
+        scores = []
+        for n in range(MOVE_TILES):
+            scores.append(sbuf([P, COLUMNS], F32, "scores_%d" % n, "page", PAGE_BUFS))
+            moves = slice(n * P, (n + 1) * P)
             for c in range(CHUNKS):
-                bank = psum.tile([P, BANK], F32, name="bank", tag="bank_%d" % (CHUNKS * (n % 2) + c))
+                bank = psum_bank(CHUNKS * (n % 2) + c)
                 for a in range(2):
                     nc.tensor.matmul_mx(
-                        out=bank[:], lhsT=v2[:, a, ns].bitcast(FP8X4), lhsT_scale=v2_sc[4 * a:P, ns],
+                        out=bank[:], lhsT=v2[:, a, moves].bitcast(FP8X4), lhsT_scale=v2_sc[4 * a:P, moves],
                         rhs=codes[(a, c)].bitcast(FP8X4), rhs_scale=scales[(a, c)][:],
                         start=(a == 0), stop=(a == 1),
                     )
-                copy_on("vector" if (n, c) in VCOPY else "scalar", e[n][:, c * BANK:(c + 1) * BANK], bank[:])
+                copy_on((n, c) not in VECTOR_BANKS, scores[n][:, c * BANK:(c + 1) * BANK], bank[:])
 
-        def finish(n):
-            picked = sbuf([P, P_OUT], F32, "picked_%d" % n, PICK_TAG[n])
-            edges = [0, BANK, P_OUT] if n + 1 < S2 // P else LAST_EDGES
+        for n in range(MOVE_TILES):
+            picked = sbuf([P, PICKS], F32, "picked_%d" % n, PICK_TAG[n])
+            edges = [0, BANK, PICKS] if n + 1 < MOVE_TILES else LAST_EDGES
             for lo, hi in zip(edges, edges[1:]):
-                gather(picked[:, lo:hi], e[n][:], idx4, lo, hi)
+                gather(picked[:, lo:hi], scores[n][:], idx4, lo, hi)
                 nc.scalar.activation(picked[:, lo:hi], picked[:, lo:hi], ACT.Sigmoid, bias=prior_sb[:, n:n + 1])
                 nc.sync.dma_start(out[n * P:(n + 1) * P, lo:hi], picked[:, lo:hi])
-
-        for n in range(S2 // P):
-            score(n)
-        for n in range(S2 // P):
-            finish(n)

from contextlib import ExitStack

import concourse.mybir as mybir
from concourse.masks import make_identity

K1, K2, H = 1024, 512, 1024
COLUMNS = 2048
BOARDS, MOVES, PICKS = 1024, 512, 1024
FLOPS = 2 * (K1 + K2) * H * BOARDS + 2 * H * MOVES * COLUMNS

F32 = mybir.dt.float32
BF16 = mybir.dt.bfloat16
I32 = mybir.dt.int32
U32 = mybir.dt.uint32
U16 = mybir.dt.uint16
U8 = mybir.dt.uint8
FP8X4 = mybir.dt.float8_e4m3fn_x4
FP4X4 = mybir.dt.float4_e2m1fn_x4
ACT = mybir.ActivationFunctionType
MULT = mybir.AluOpType.mult

P = 128
QUADRANT = 32
PACK = 4
K_PASS = P * PACK
BANK = 512
GROUP = 16
PLANES = H // P
CHUNKS = COLUMNS // BANK
MOVE_TILES = MOVES // P
W4_PASS = K1 // K_PASS
TAB_SCALE_ROW = {0: 4, 1: 8, W4_PASS: 0}

SLABS = 5
PAGE_BUFS = 5
TANH_TAG = ["tanh_%d" % b for b in (0, 1, 2, 3, 4, 0, 1, 3)]
PICK_TAG = ["tanh_%d" % b for b in (0, 1, 2, 4)]
FACTOR_TAG = ["factor_%d" % (k % 5) for k in range(PLANES)]
LAST_CODES_TAG = ("v_0", "v_1", "v_2", "wgs_sb")
H_BANKS, WGS_BANKS, FACTOR_BANKS = 0, 4, 6

SCALAR_ROUNDS = 2
SCALAR_WEAVES = 3
VECTOR_BANKS = ((0, SCALAR_WEAVES - 1), (1, SCALAR_WEAVES - 1))
LAST_EDGES = [0, 512, 768, 1024]


def tile_list_opening_explorer_scores_kernel(
    tc, tab_words, tab_scales, w1, w4_words, w4_scales, gain, page0, wgs,
    tab2_words, tab2_scales, prior, offs, offs2, offs3, offs4, out,
):
    nc = tc.nc
    with ExitStack() as ctx:
        keep = ctx.enter_context(tc.tile_pool(name="keep", bufs=1))
        psum = ctx.enter_context(tc.psum_pool(name="psum", bufs=1))

        def sbuf(shape, dtype, name, tag=None, bufs=1):
            return keep.tile(shape, dtype, name=name, tag=tag or name, bufs=bufs, align_bytes=64)

        def psum_bank(number):
            return psum.tile([P, BANK], F32, name="bank", tag="bank_%d" % number)

        def copy_on(on_scalar, dst, src):
            if on_scalar:
                nc.scalar.copy(dst, src)
            else:
                nc.vector.tensor_copy(dst, src)

        def load_list(src, name):
            offsets = keep.tile(list(src.shape), U16, name=name, tag=name)
            nc.sync.dma_start(offsets[:], src)
            return offsets

        def load_words(words, a, name):
            window = sbuf([P, COLUMNS], I32, name, "slab", SLABS)
            nc.sync.dma_start(window[:], words[a].rearrange("p t i -> p (t i)").bitcast(I32))
            return window

        def load_w1(a, g):
            raw = sbuf([P, PACK, K_PASS], F32, "w1_raw_%d_%d" % (a, g), "slab", SLABS)
            rows = w1[g * K_PASS:(g + 1) * K_PASS, a * K_PASS:(a + 1) * K_PASS]
            nc.sync.dma_start(raw[:], rows.rearrange("(p j) c -> p j c", j=PACK))
            return raw

        def load_page(k):
            a, i = divmod(k, PACK)
            plane = sbuf([P, COLUMNS], F32, "page_%d" % k, "page", PAGE_BUFS)
            rows = page0[a * K_PASS:(a + 1) * K_PASS, :].rearrange("(p i) t -> p i t", i=PACK)
            nc.sync.dma_start(plane[:], rows[:, i, :])
            return plane

        def scale_tile(width, name):
            rows = sbuf([P, width], U8, name)
            nc.vector.memset(rows[:].bitcast(I32), 0)
            return rows

        def load_scales(queue, dst, scales, first, count, row):
            for quad in range(P // QUADRANT):
                base = QUADRANT * quad + row
                queue.dma_start(
                    dst[base:base + 4 * count, :].bitcast(I32),
                    scales[first:first + count, 4 * quad:4 * quad + 4, :].bitcast(I32),
                )

        def gather(dst, window, offsets, lo, hi):
            nc.vector.tensor_copy(dst, window.indirect(offsets[:, lo // GROUP:hi // GROUP]))

        tab_sc = scale_tile(COLUMNS, "tab_sc")
        w4_sc_raw = scale_tile(H, "w4_sc_raw")
        tab2_sc = scale_tile(COLUMNS, "tab2_sc")
        identity = sbuf([P, P], F32, "identity")
        make_identity(nc, identity[:])

        idx = load_list(offs, "idx")
        tab = {W4_PASS: load_words(tab_words, W4_PASS, "tab_2")}
        load_scales(nc.gpsimd, tab_sc, tab_scales, 0, 2, TAB_SCALE_ROW[0])
        w4_raw = sbuf([P, 2 * H], U8, "w4_raw")
        nc.sync.dma_start(w4_raw[:].bitcast(I32), w4_words[0].bitcast(I32))
        wgs_sb = sbuf([P, BOARDS], F32, "wgs_sb")
        nc.sync.dma_start(wgs_sb[:], wgs)
        tab[0] = load_words(tab_words, 0, "tab_0")
        load_scales(nc.sync, tab_sc, tab_scales, W4_PASS, 1, TAB_SCALE_ROW[W4_PASS])
        w1_raw = {(0, 0): load_w1(0, 0)}
        load_scales(nc.sync, w4_sc_raw, w4_scales, 0, 1, 0)
        gain_sb = sbuf([P, 2, PACK], F32, "gain_sb")
        nc.scalar.dma_start(gain_sb[:], gain.rearrange("(a p i) -> p a i", p=P, i=PACK))
        w1_raw[(0, 1)] = load_w1(0, 1)
        tab[1] = load_words(tab_words, 1, "tab_1")
        idx3 = load_list(offs3, "idx3")
        w4 = sbuf([P, 2 * H], U8, "w4")
        nc.vector.tensor_copy(
            w4[:].bitcast(U16).rearrange("p (a i m) -> p a i m", a=2, i=PACK),
            w4_raw[:].bitcast(U16).rearrange("p (a m i) -> p a i m", a=2, i=PACK),
        )
        page = [load_page(0)]
        w1_raw[(1, 0)] = load_w1(1, 0)
        page.append(load_page(1))
        w1_raw[(1, 1)] = load_w1(1, 1)
        page.append(load_page(2))
        idx2 = load_list(offs2, "idx2")
        load_scales(nc.sync, tab2_sc, tab2_scales, 0, 2, 0)
        idx4 = load_list(offs4, "idx4")
        prior_sb = sbuf([P, MOVE_TILES], F32, "prior_sb")
        with nc.allow_non_contiguous_dma(reason="one prior value for each partition"):
            nc.sync.dma_start(prior_sb[:], prior.rearrange("(n p) -> p n", p=P))
        tab2 = [load_words(tab2_words, a, "tab2_%d" % a) for a in range(2)]
        for k in range(3, PLANES):
            page.append(load_page(k))

        v = {g: sbuf([P, BOARDS], U32, "v_%d" % g) for g in range(3)}
        v_sc = sbuf([P, BOARDS], U8, "v_sc")
        w1_codes, w1_sc = {}, {}

        def weave_w1(a, g, tag, first=0, last=PACK):
            woven_w1 = sbuf([P, last - first, K_PASS], BF16, "w1_woven", tag)
            nc.scalar.copy(
                woven_w1[:].rearrange("p i (m j) -> p m j i", j=PACK),
                w1_raw[(a, g)][:].rearrange("p j (m i) -> p m j i", i=PACK)[:, :, :, first:last],
            )
            return woven_w1[:]

        def quantize_w1(a, g, woven_w1, first=0):
            if first == 0:
                w1_sc[(a, g)] = sbuf([P, K_PASS], U8, "w1_sc_%d_%d" % (a, g))
            cols = slice(first * P, (first + woven_w1.shape[1]) * P)
            nc.vector.quantize_mx(
                out=w1_codes[a][:, g, cols].bitcast(FP8X4), scales=w1_sc[(a, g)][:, cols],
                in_=woven_w1.rearrange("p i c -> p (i c)"),
            )

        def turn(src, first_bank):
            banks = []
            for b in range(2):
                bank = psum_bank(first_bank + b)
                for c in range(BANK // P):
                    col = b * BANK + c * P
                    nc.tensor.transpose(bank[:, c * P:(c + 1) * P], src[:, col:col + P], identity[:])
                banks.append(bank)
            return banks

        wgs_turned = turn(wgs_sb, WGS_BANKS)
        spread = {}

        def spread_rows(i, dst):
            spread[i] = dst
            for b in range(2):
                rows = wgs_turned[b][:].rearrange("p (c q i) -> p c q i", q=QUADRANT, i=PACK)[:, :, :, i]
                nc.scalar.copy(
                    dst[:, b * BANK:(b + 1) * BANK].rearrange("p (c g q) -> p c g q", g=P // QUADRANT, q=QUADRANT),
                    rows.unsqueeze(2).to_broadcast([P, BANK // P, P // QUADRANT, QUADRANT]),
                )

        spread_rows(0, sbuf([P, BOARDS], F32, "spread_0")[:])
        gather(v[W4_PASS][:], tab[W4_PASS][:].bitcast(U32), idx, 0, BOARDS)
        gather(v[0][:], tab[0][:].bitcast(U32), idx, 0, BOARDS)
        gather(v_sc[:], tab_sc[:], idx, 0, BOARDS)
        first_w1 = weave_w1(0, 0, "woven_0")
        w1_codes[0] = sbuf([P, 2, K_PASS], U32, "w1_codes_0")
        quantize_w1(0, 0, first_w1)
        w4_sc = sbuf([P, H], U8, "w4_sc")
        nc.vector.tensor_copy(
            w4_sc[:].rearrange("p (a i m) -> p a i m", a=2, i=PACK),
            w4_sc_raw[:].rearrange("p (a m i) -> p a i m", a=2, i=PACK),
        )
        quantize_w1(0, 1, weave_w1(0, 1, "spread_rest", 0, 1))
        rest_w1 = weave_w1(0, 1, "spread_rest", 1, PACK)
        for lo in range(0, BOARDS, BANK):
            gather(v[1][:, lo:lo + BANK], tab[1][:].bitcast(U32), idx, lo, lo + BANK)
        quantize_w1(0, 1, rest_w1[:, 0:1, :], 1)
        quantize_w1(0, 1, rest_w1[:, 1:3, :], 2)

        tanh_sb, factor = {}, {}

        def make_factors(i, passes):
            banks = turn(spread[i], FACTOR_BANKS)
            for a in passes:
                k = a * PACK + i
                factor[k] = sbuf([P, BOARDS], F32, "factor_%d" % k, FACTOR_TAG[k])
                for b, bank in enumerate(banks):
                    nc.scalar.activation(
                        factor[k][:, b * BANK:(b + 1) * BANK], bank[:], ACT.Copy, scale=gain_sb[:, a, i:i + 1]
                    )

        def encode(k):
            a, i = divmod(k, PACK)
            tanh_sb[k] = sbuf([P, BOARDS], F32, "tanh_%d" % k, TANH_TAG[k])
            plane_cols = slice(i * P, (i + 1) * P)
            col = a * K_PASS + i * P
            first_bank = WGS_BANKS if k % 2 and k > 1 else H_BANKS
            for lo in range(0, BOARDS, BANK):
                js = slice(lo, lo + BANK)
                bank = psum_bank(first_bank + lo // BANK)
                for g in (0, W4_PASS, 1):
                    if g == W4_PASS:
                        lhs, lhs_sc = w4[:, 2 * col:2 * (col + P)].bitcast(FP4X4), w4_sc[:, col:col + P]
                    else:
                        lhs, lhs_sc = w1_codes[a][:, g, plane_cols].bitcast(FP8X4), w1_sc[(a, g)][:, plane_cols]
                    nc.tensor.matmul_mx(
                        out=bank[:], lhsT=lhs, lhsT_scale=lhs_sc,
                        rhs=v[g][:, js].bitcast(FP8X4), rhs_scale=v_sc[TAB_SCALE_ROW[g]:P, js],
                        start=(g == 0), stop=(g == 1),
                    )
                nc.scalar.activation(tanh_sb[k][:, js], bank[:], ACT.Tanh)

        def scatter(k, step=BOARDS):
            for lo in range(0, BOARDS, step):
                nc.vector.tensor_tensor(
                    page[k][:].indirect(idx3[:, lo // GROUP:(lo + step) // GROUP]),
                    tanh_sb[k][:, lo:lo + step], factor[k][:, lo:lo + step], MULT,
                )

        rounded, woven, codes, scales = {}, {}, {}, {}

        def round_plane(k, scalar_chunks=CHUNKS):
            a, i = divmod(k, PACK)
            for c in range(CHUNKS):
                if i == 0:
                    rounded[(a, c)] = sbuf([P, PACK, BANK], BF16, "rounded_%d_%d" % (a, c), "rounded_%d" % c)
                copy_on(c < scalar_chunks, rounded[(a, c)][:, i, :], page[k][:, c * BANK:(c + 1) * BANK])

        def weave(a, c, on_scalar=True):
            woven[(a, c)] = sbuf([P, PACK * BANK], BF16, "woven_%d_%d" % (a, c), "woven_%d" % (CHUNKS * a + c))
            copy_on(
                on_scalar,
                woven[(a, c)][:].rearrange("p (t i) -> p t i", i=PACK),
                rounded[(a, c)][:].rearrange("p i t -> p t i"),
            )

        def quantize_page(a, c, dst):
            codes[(a, c)] = dst
            scales[(a, c)] = sbuf([P, BANK], U8, "page_sc_%d_%d" % (a, c))
            nc.vector.quantize_mx(out=dst.bitcast(FP8X4), scales=scales[(a, c)][:], in_=woven[(a, c)][:])

        make_factors(0, (0, 1))
        encode(0)
        spread_rest = sbuf([P, PACK - 1, BOARDS], F32, "spread_rest")
        for i in (1, 2):
            spread_rows(i, spread_rest[:, i - 1, :])
            make_factors(i, (0,))
            encode(i)
        scatter(0, BANK)
        spread_rows(3, spread_rest[:, 2, :])
        make_factors(3, (0,))
        encode(3)
        late_w1 = [weave_w1(1, g, "woven_%d" % (2 + g)) for g in range(2)]
        for k in (1, 2):
            scatter(k)
            round_plane(k - 1)
        w1_codes[1] = sbuf([P, 2, K_PASS], U32, "w1_codes_1", TANH_TAG[2])
        for g in range(2):
            quantize_w1(1, g, late_w1[g])
        v2_sc = sbuf([P, MOVES], U8, "v2_sc")
        gather(v2_sc[:], tab2_sc[:], idx2, 0, MOVES)
        round_plane(2)
        encode(4)
        scatter(3)
        make_factors(1, (1,))
        encode(5)
        scatter(4)
        round_plane(3)
        weave(0, 0)
        make_factors(2, (1,))
        encode(6)
        scatter(5)
        weave(0, 1)
        weave(0, 2)
        make_factors(3, (1,))
        encode(7)
        scatter(6)
        weave(0, 3)
        round_plane(4)
        scatter(7)
        round_plane(5)
        round_plane(6)

        round_plane(7, SCALAR_ROUNDS)
        for c in range(SCALAR_WEAVES):
            weave(1, c)
        v2 = sbuf([P, 2, MOVES], U32, "v2", TANH_TAG[7])
        for a in range(2):
            gather(v2[:, a, :], tab2[a][:].bitcast(U32), idx2, 0, MOVES)
        first_codes = sbuf([P, COLUMNS], U32, "page_codes_0", FACTOR_TAG[7])
        for c in range(CHUNKS):
            if c >= SCALAR_WEAVES:
                weave(1, c, on_scalar=False)
            quantize_page(0, c, first_codes[:, c * BANK:(c + 1) * BANK])
            quantize_page(1, c, sbuf([P, BANK], U32, "page_codes_1_%d" % c, LAST_CODES_TAG[c])[:])

        scores = []
        for n in range(MOVE_TILES):
            scores.append(sbuf([P, COLUMNS], F32, "scores_%d" % n, "page", PAGE_BUFS))
            moves = slice(n * P, (n + 1) * P)
            for c in range(CHUNKS):
                bank = psum_bank(CHUNKS * (n % 2) + c)
                for a in range(2):
                    nc.tensor.matmul_mx(
                        out=bank[:], lhsT=v2[:, a, moves].bitcast(FP8X4), lhsT_scale=v2_sc[4 * a:P, moves],
                        rhs=codes[(a, c)].bitcast(FP8X4), rhs_scale=scales[(a, c)][:],
                        start=(a == 0), stop=(a == 1),
                    )
                copy_on((n, c) not in VECTOR_BANKS, scores[n][:, c * BANK:(c + 1) * BANK], bank[:])

        for n in range(MOVE_TILES):
            picked = sbuf([P, PICKS], F32, "picked_%d" % n, PICK_TAG[n])
            edges = [0, BANK, PICKS] if n + 1 < MOVE_TILES else LAST_EDGES
            for lo, hi in zip(edges, edges[1:]):
                gather(picked[:, lo:hi], scores[n][:], idx4, lo, hi)
                nc.scalar.activation(picked[:, lo:hi], picked[:, lo:hi], ACT.Sigmoid, bias=prior_sb[:, n:n + 1])
                nc.sync.dma_start(out[n * P:(n + 1) * P, lo:hi], picked[:, lo:hi])
